import numpy as np
import ml_dtypes


def mxq(x, axis, fmt="e4m3"):
    dtype, down = {"e4m3": (ml_dtypes.float8_e4m3fn, 7), "e5m2": (ml_dtypes.float8_e5m2, 14)}[fmt]
    v = np.moveaxis(np.asarray(x, np.float32).astype(ml_dtypes.bfloat16).astype(np.float64), axis, -1)
    blocks = v.reshape(v.shape[:-1] + (-1, 32))
    amax = np.abs(blocks).max(-1, keepdims=True)
    byte = np.maximum(np.where(amax > 0, np.frexp(amax)[1] - 1 + 127, 0) - down, 1)
    scale = np.exp2(byte - 127.0)
    codes = (blocks / scale).astype(np.float32).astype(dtype).astype(np.float64)
    return np.moveaxis((codes * scale).reshape(v.shape), -1, axis)


WIDE = False


def mx_kscale(k):
    if not WIDE:
        return np.ones(k)
    levels = np.array([10, -10, 5, -5, 0])
    if k % 512:
        return np.exp2(np.random.permutation(np.resize(levels, k // 32))).repeat(32)
    a = np.empty((k // 512, 16))
    for p in range(k // 512):
        a[p, :8] = np.random.permutation(np.resize(levels, 8))
        for g in range(8):
            far = levels[np.abs(levels - a[p, g]) >= 10]
            a[p, g + 8] = far[np.random.randint(len(far))]
    return np.exp2(a.ravel()).repeat(32)


def f64(x):
    return np.asarray(x).astype(np.float64)


def striped(idx):
    return np.tile(idx.reshape(-1, 16).T, (8, 1)).astype(np.uint16)


def unstriped(offs):
    return offs[:16].T.reshape(-1).astype(np.int64)


E2M1 = np.array([0.0, 0.5, 1.0, 1.5, 2.0, 3.0, 4.0, 6.0, -0.0, -0.5, -1.0, -1.5, -2.0, -3.0, -4.0, -6.0])


def pack_weight(w, fmt):
    k, n = w.shape
    w = f64(np.asarray(w, np.float32).astype(ml_dtypes.bfloat16)).reshape(k // 32, 32, n)
    amax = np.abs(w).max(1)
    if fmt == "e4m3":
        byte = np.frexp(amax)[1] - 1 + 127 - 7
    else:
        mant, ex = np.frexp(amax / 6.0)
        byte = np.where(mant > 0.5, ex, ex - 1) + 127
    byte = np.clip(np.where(amax > 0, byte, 1), 1, 254)
    scaled = (w * np.exp2(127.0 - byte)[:, None, :]).reshape(k, n).astype(np.float32)
    by_word = np.ascontiguousarray(scaled.reshape(k // 512, 128, 4, n).transpose(0, 1, 3, 2))
    if fmt == "e4m3":
        words = by_word.astype(ml_dtypes.float8_e4m3fn).view(np.uint8)
    else:
        c = by_word.astype(ml_dtypes.float4_e2m1fn).view(np.uint8) & 0xF
        words = (c[..., 0::2] | (c[..., 1::2] << 4)).reshape(k // 512, 128, 2 * n)
    return np.ascontiguousarray(words), np.ascontiguousarray(byte.astype(np.uint8).reshape(k // 512, 16, n))


def unpack_weight(words, scales, fmt):
    g, _, n = scales.shape
    words = np.ascontiguousarray(words).reshape(g, 128, n, -1)
    if fmt == "e4m3":
        vals = words.view(ml_dtypes.float8_e4m3fn).astype(np.float64)
    else:
        nib = np.empty((g, 128, n, 4), np.uint8)
        nib[..., 0::2] = words & 0xF
        nib[..., 1::2] = words >> 4
        vals = E2M1[nib]
    vals = vals * np.repeat(np.exp2(scales.astype(np.float64) - 127.0), 8, axis=1)[..., None]
    return vals.transpose(0, 1, 3, 2).reshape(g * 512, n)


def sigmoid(v):
    return 1.0 / (1.0 + np.exp(-np.maximum(v, -700.0)))


K, T, E, C, H, N = 512, 2560, 6, 256, 512, 512
R = 4


def by_expert(wq, xq):
    return np.concatenate([wq[e].T @ xq[:, e * C:(e + 1) * C] for e in range(E)], axis=1)


def setup_inputs():
    n = np.random.standard_normal
    s = mx_kscale(K)[:, None]
    u = mx_kscale(H)
    slot_token = np.concatenate([r * (T // R) + np.random.permutation(T // R)[:C // R] for e in range(E) for r in range(R)])
    w1 = [pack_weight(m, "e2m1") for m in n((E, K, H)) / np.sqrt(K) / s[None]]
    w3 = [pack_weight(m, "e2m1") for m in n((E, K, H)) / np.sqrt(K) / s[None] * u[None, None, :]]
    w2 = [pack_weight(m, "e2m1") for m in n((E, H, N)) / np.sqrt(H) / u[None, :, None]]
    x = pack_weight(n((K, T)) * s, "e4m3")
    return {
        "x_words": x[0],
        "x_scales": x[1],
        "w1_words": np.stack([m[0] for m in w1]),
        "w1_scales": np.stack([m[1] for m in w1]),
        "w3_words": np.stack([m[0] for m in w3]),
        "w3_scales": np.stack([m[1] for m in w3]),
        "w2_words": np.stack([m[0] for m in w2]),
        "w2_scales": np.stack([m[1] for m in w2]),
        "offs": striped(slot_token),
    }


def reference(x_words, x_scales, w1_words, w1_scales, w3_words, w3_scales, w2_words, w2_scales, offs):
    idx = unstriped(offs)
    w1 = np.stack([unpack_weight(w1_words[e], w1_scales[e], "e2m1") for e in range(E)])
    w3 = np.stack([unpack_weight(w3_words[e], w3_scales[e], "e2m1") for e in range(E)])
    w2 = np.stack([unpack_weight(w2_words[e], w2_scales[e], "e2m1") for e in range(E)])
    xq = unpack_weight(x_words, x_scales, "e4m3")[:, idx]
    h = sigmoid(by_expert(w1, xq))
    h = h * by_expert(w3, xq)
    y = by_expert(w2, mxq(h, 0, "e4m3"))
    return y.reshape(N, E, R, C // R).transpose(0, 2, 1, 3).reshape(N, E * C)

@@ -1,0 +1,343 @@
+from contextlib import ExitStack
+
+import concourse.mybir as mybir
+from concourse.masks import make_identity
+
+K, T, E, C, H, N, R = 512, 2560, 6, 256, 512, 512, 4
+S = E * C
+FLOPS = 2 * S * (2 * K * H + H * N)
+
+F32 = mybir.dt.float32
+BF16 = mybir.dt.bfloat16
+I32 = mybir.dt.int32
+U32 = mybir.dt.uint32
+U16 = mybir.dt.uint16
+U8 = mybir.dt.uint8
+FP8X4 = mybir.dt.float8_e4m3fn_x4
+FP4X4 = mybir.dt.float4_e2m1fn_x4
+SIGMOID = mybir.ActivationFunctionType.Sigmoid
+MULT = mybir.AluOpType.mult
+
+P = 128
+WORD_CUTS = [512,512,512]
+SCALE_CUTS = [384,384,384,384]
+SCALE_TAGS = [0,1,0,1]
+BANKS = [0,1,2,3,4,5,6,7,0,1,2,3,4,5,6,7,0,1,2,3,4,5,6,7,0,1,2,3,4,5,6,7,0,1,2,3,4,5,6,7,0,1,2,3]
+
+
+def tile_moe_pke_glu_sigmoid_kernel(
+    tc, x_words, x_scales, w1_words, w1_scales, w3_words, w3_scales, w2_words, w2_scales, offs, out
+):
+    nc = tc.nc
+    with ExitStack() as ctx:
+        keep = ctx.enter_context(tc.tile_pool(name="keep", bufs=1))
+        ring_gw = ctx.enter_context(tc.tile_pool(name="ring_gw", bufs=4))
+        ring_sig = ctx.enter_context(tc.tile_pool(name="ring_sig", bufs=3))
+        ring_h = ctx.enter_context(tc.tile_pool(name="ring_h", bufs=3))
+        ring_ht = ctx.enter_context(tc.tile_pool(name="ring_ht", bufs=3))
+        ring_q = ctx.enter_context(tc.tile_pool(name="ring_q", bufs=4))
+        psum = ctx.enter_context(tc.psum_pool(name="psum", bufs=1))
+
+        offsets = keep.tile([P, S // 16], U16, name="offsets")
+        xw = keep.tile([P, T], I32, name="xw", align_bytes=64)
+        xs = keep.tile([P, T // 4], I32, name="xs", align_bytes=64)
+        ident = keep.tile([P, P], F32, name="ident", align_bytes=64)
+        warm = keep.tile([P, 1], F32, name="warm")
+        words = {}
+        planes = {}
+        for name in ("w1", "w3", "w2"):
+            words[name] = keep.tile([P, E * 1024], U8, name=name + "_words", align_bytes=64)
+            planes[name] = keep.tile([P, E * 512], U8, name=name + "_plane", align_bytes=64)
+        dram_words = {"w1": w1_words, "w3": w3_words, "w2": w2_words}
+        dram_scales = {"w1": w1_scales, "w3": w3_scales, "w2": w2_scales}
+
+        def load_words(queue, name, e0, e1):
+            queue.dma_start(
+                words[name][:, e0 * 1024 : e1 * 1024].bitcast(I32).rearrange("p (e w) -> p e w", e=e1 - e0),
+                dram_words[name][e0:e1, 0].rearrange("e p b -> p e b").bitcast(I32),
+            )
+
+        def load_scales(queue, name, e0, e1):
+            for j in range(4):
+                queue.dma_start(
+                    planes[name][j:P:32, e0 * 512 : e1 * 512].bitcast(I32).rearrange("p (e w) -> p e w", e=e1 - e0),
+                    dram_scales[name][e0:e1, 0, j:16:4, :].rearrange("e q b -> q e b").bitcast(I32),
+                )
+
+        def load_xs(queue):
+            for j in range(4):
+                queue.dma_start(xs[j:P:32, :], x_scales[0, j:16:4, :].bitcast(I32))
+
+        def load_xw(queue):
+            queue.dma_start(xw[:], x_words[0].rearrange("p t r -> p (t r)").bitcast(I32))
+
+        def zero(engine, name, e0, e1):
+            engine.memset(planes[name][:, e0 * 512 : e1 * 512].bitcast(I32), 0)
+
+        load_xw(nc.gpsimd)
+        nc.vector.memset(warm[:], 0.0)
+        nc.vector.memset(xs[:], 0)
+        zero(nc.vector, "w1", 0, 2)
+        zero(nc.vector, "w3", 0, 2)
+        zero(nc.vector, "w2", 0, E)
+        zero(nc.vector, "w1", 2, E)
+        zero(nc.vector, "w3", 2, E)
+        nc.scalar.activation(warm[:], warm[:], SIGMOID)
+        nc.sync.dma_start(offsets[:], offs)
+        load_xs(nc.sync)
+        load_words(nc.gpsimd, "w1", 0, 2)
+        load_words(nc.gpsimd, "w3", 0, 2)
+        make_identity(nc, ident[:])
+        load_words(nc.gpsimd, "w2", 0, 2)
+        load_words(nc.gpsimd, "w1", 2, E)
+        load_words(nc.gpsimd, "w3", 2, E)
+        load_words(nc.gpsimd, "w2", 2, E)
+        load_scales(nc.sync, "w1", 0, 2)
+        load_scales(nc.sync, "w3", 0, 2)
+        load_scales(nc.sync, "w2", 0, E)
+        load_scales(nc.sync, "w1", 2, E)
+        load_scales(nc.sync, "w3", 2, E)
+
+        gathered_words = {}
+        gathered_scales = {}
+
+        def gather_words(g):
+            s0 = sum(WORD_CUTS[:g])
+            n = WORD_CUTS[g]
+            tile = ring_gw.tile([P, n], I32, name="gw", align_bytes=64)
+            nc.vector.tensor_copy(
+                tile[:].bitcast(U32), xw[:].bitcast(U32).indirect(offsets[:, s0 // 16 : (s0 + n) // 16])
+            )
+            for u in range(n // P):
+                gathered_words[s0 // P + u] = tile[:, u * P : (u + 1) * P]
+
+        def gather_scales(g):
+            s0 = sum(SCALE_CUTS[:g])
+            n = SCALE_CUTS[g]
+            tile = keep.tile([P, n], U8, name="gs%d" % SCALE_TAGS[g], align_bytes=64)
+            nc.vector.tensor_copy(tile[:], xs[:].bitcast(U8).indirect(offsets[:, s0 // 16 : (s0 + n) // 16]))
+            for u in range(n // P):
+                gathered_scales[s0 // P + u] = tile[:, u * P : (u + 1) * P]
+
+        held = {}
+        taken = []
+
+        def bank(kind, shape):
+            taken.append(kind)
+            return psum.tile(shape, F32, name="bank%d" % BANKS[len(taken) - 1])
+
+        def copy(engine, dst, src):
+            if engine == "V":
+                nc.vector.tensor_copy(dst, src)
+            else:
+                nc.scalar.copy(dst, src)
+
+        def first(kind, u):
+            e = u // 2
+            name = {"a": "w1", "b": "w3"}[kind]
+            acc = bank(kind, [P, H])
+            nc.tensor.matmul_mx(
+                acc[:],
+                lhsT=gathered_words[u].bitcast(FP8X4),
+                lhsT_scale=gathered_scales[u],
+                rhs=words[name][:, e * 1024 : (e + 1) * 1024].bitcast(FP4X4),
+                rhs_scale=planes[name][:, e * 512 : (e + 1) * 512],
+                start=True,
+                stop=True,
+            )
+            held[kind, u] = acc
+
+        def sigmoid(u):
+            sig = ring_sig.tile([P, H], F32, name="sig", align_bytes=64)
+            nc.scalar.activation(
+                sig[:].rearrange("s (v p d) -> s v p d", v=2, d=2),
+                held["a", u][:].rearrange("s (p v d) -> s v p d", v=2, d=2),
+                SIGMOID,
+            )
+            held["sig", u] = sig
+
+        def gate(u):
+            h = ring_h.tile([P, H], BF16, name="h", align_bytes=64)
+            nc.vector.tensor_tensor(
+                h[:].rearrange("s (v p d) -> s v p d", v=2, d=2),
+                held["b", u][:].rearrange("s (p v d) -> s v p d", v=2, d=2),
+                held["sig", u][:].rearrange("s (v p d) -> s v p d", v=2, d=2),
+                MULT,
+            )
+            held["h", u] = h
+
+        def turn(us):
+            turned = bank("t", [P, len(us), 2, P])
+            for half, u in enumerate(us):
+                pairs = held["h", u][:].bitcast(F32)
+                for v in range(2):
+                    nc.tensor.transpose(turned[:, half, v, :], pairs[:, v * P : (v + 1) * P], ident[:])
+            held["t", us[0]] = turned
+
+        def collect(us, engine):
+            ht = ring_ht.tile([P, 4 * P * len(us)], BF16, name="ht", align_bytes=64)
+            dst = ht[:].bitcast(F32).rearrange("p (a s v) -> p a s v", a=len(us), v=2)
+            copy(engine, dst, held["t", us[0]][:].rearrange("p a v s -> p a s v"))
+            held["ht", us[0]] = ht
+
+        def quantise(us):
+            codes = ring_q.tile([P, P * len(us)], U32, name="codes", align_bytes=64)
+            scales = ring_q.tile([P, P * len(us)], U8, name="scales", align_bytes=64)
+            nc.vector.quantize_mx(codes[:].bitcast(FP8X4), scales[:], held["ht", us[0]][:])
+            held["q", us[0]] = (codes, scales)
+
+        def second(us, ts):
+            e = us[0] // 2
+            codes, scales = held["q", us[0]]
+            y = bank("y", [P, len(ts), P * len(us)])
+            for k, t in enumerate(ts):
+                nc.tensor.matmul_mx(
+                    y[:, k, :],
+                    lhsT=words["w2"][:, e * 1024 + t * 256 : e * 1024 + (t + 1) * 256].bitcast(FP4X4),
+                    lhsT_scale=planes["w2"][:, e * 512 + t * P : e * 512 + (t + 1) * P],
+                    rhs=codes[:].bitcast(FP8X4),
+                    rhs_scale=scales[:],
+                    start=True,
+                    stop=True,
+                )
+            held["y", us[0], ts[0]] = y
+
+        result = keep.tile([P, 4, R, E * 64], F32, name="result", align_bytes=64)
+        rows = out.rearrange("(t p) (m c) -> p t m c", p=P, m=R)
+
+        def empty(us, ts, engine):
+            e = us[0] // 2
+            m0 = 2 * (us[0] % 2)
+            dst = result[:, ts[0] : ts[-1] + 1, m0 : m0 + 2 * len(us), 64 * e : 64 * e + 64]
+            copy(engine, dst, held["y", us[0], ts[0]][:].rearrange("p k (m c) -> p k m c", c=64))
+
+        def store(queue, t0, t1, m0, m1, e0, e1):
+            if t1 - t0 == 1:
+                queue.dma_start(rows[:, t0, m0:m1, 64 * e0 : 64 * e1], result[:, t0, m0:m1, 64 * e0 : 64 * e1])
+            else:
+                queue.dma_start(rows[:, t0:t1, m0, 64 * e0 : 64 * e1], result[:, t0:t1, m0, 64 * e0 : 64 * e1])
+
+        gather_scales(0)
+        gather_words(0)
+        gather_scales(1)
+        first("a", 0)
+        first("a", 1)
+        first("b", 0)
+        sigmoid(0)
+        gate(0)
+        gather_words(1)
+        first("a", 2)
+        first("b", 1)
+        sigmoid(1)
+        gate(1)
+        first("a", 3)
+        first("b", 2)
+        sigmoid(2)
+        gate(2)
+        first("a", 4)
+        first("b", 3)
+        sigmoid(3)
+        gate(3)
+        turn([0,1])
+        first("a", 5)
+        first("b", 4)
+        sigmoid(4)
+        collect([0,1], "A")
+        quantise([0,1])
+        gather_scales(2)
+        gate(4)
+        first("a", 6)
+        first("b", 5)
+        sigmoid(5)
+        gather_words(2)
+        gate(5)
+        turn([2,3])
+        second([0,1], [0,1])
+        first("a", 7)
+        first("b", 6)
+        sigmoid(6)
+        collect([2,3], "A")
+        quantise([2,3])
+        second([0,1], [2,3])
+        gate(6)
+        empty([0,1], [0,1], "V")
+        first("a", 8)
+        first("b", 7)
+        sigmoid(7)
+        empty([0,1], [2,3], "A")
+        gather_scales(3)
+        gate(7)
+        turn([4,5])
+        second([2,3], [0,1])
+        empty([2,3], [0,1], "A")
+        store(nc.sync, 0, 1, 0, 4, 0, 2)
+        store(nc.sync, 1, 2, 0, 4, 0, 2)
+        first("a", 9)
+        first("b", 8)
+        sigmoid(8)
+        collect([4,5], "V")
+        quantise([4,5])
+        second([2,3], [2,3])
+        empty([2,3], [2,3], "A")
+        store(nc.sync, 2, 3, 0, 4, 0, 2)
+        store(nc.sync, 3, 4, 0, 4, 0, 2)
+        gate(8)
+        turn([6,7])
+        first("a", 10)
+        first("b", 9)
+        sigmoid(9)
+        collect([6,7], "V")
+        gate(9)
+        quantise([6,7])
+        second([4,5], [0,1])
+        first("a", 11)
+        first("b", 10)
+        sigmoid(10)
+        second([4,5], [2,3])
+        gate(10)
+        empty([4,5], [0,1], "A")
+        store(nc.sync, 0, 1, 0, 4, 2, 3)
+        store(nc.sync, 1, 2, 0, 4, 2, 3)
+        first("b", 11)
+        sigmoid(11)
+        turn([8,9])
+        second([6,7], [0,1])
+        empty([4,5], [2,3], "V")
+        store(nc.sync, 2, 3, 0, 4, 2, 3)
+        store(nc.sync, 3, 4, 0, 4, 2, 3)
+        gate(11)
+        collect([8,9], "A")
+        second([6,7], [2,3])
+        turn([10])
+        quantise([8,9])
+        empty([6,7], [0,1], "A")
+        store(nc.sync, 0, 1, 0, 4, 3, 4)
+        store(nc.sync, 1, 2, 0, 4, 3, 4)
+        turn([11])
+        collect([10], "V")
+        empty([6,7], [2,3], "A")
+        store(nc.sync, 2, 3, 0, 4, 3, 4)
+        store(nc.sync, 3, 4, 0, 4, 3, 4)
+        collect([11], "A")
+        quantise([11])
+        quantise([10])
+        second([11], [0,1])
+        second([8,9], [0,1])
+        second([10], [0,1,2,3])
+        second([11], [2,3])
+        second([8,9], [2,3])
+        empty([11], [0,1], "A")
+        store(nc.sync, 0, 2, 2, 3, 5, 6)
+        store(nc.sync, 0, 2, 3, 4, 5, 6)
+        empty([8,9], [0,1], "V")
+        empty([10], [0,1,2,3], "V")
+        empty([11], [2,3], "V")
+        store(nc.sync, 0, 1, 0, 4, 4, 5)
+        store(nc.sync, 1, 2, 0, 4, 4, 5)
+        store(nc.sync, 0, 4, 0, 1, 5, 6)
+        store(nc.sync, 0, 4, 1, 2, 5, 6)
+        store(nc.sync, 2, 4, 2, 3, 5, 6)
+        store(nc.sync, 2, 4, 3, 4, 5, 6)
+        empty([8,9], [2,3], "A")
+        store(nc.sync, 2, 3, 0, 4, 4, 5)
+        store(nc.sync, 3, 4, 0, 4, 4, 5)

@@ -19,10 +19,10 @@ SIGMOID = mybir.ActivationFunctionType.Sigmoid
 MULT = mybir.AluOpType.mult
 
 P = 128
-WORD_CUTS = [512,512,512]
-SCALE_CUTS = [384,384,384,384]
-SCALE_TAGS = [0,1,0,1]
-BANKS = [0,1,2,3,4,5,6,7,0,1,2,3,4,5,6,7,0,1,2,3,4,5,6,7,0,1,2,3,4,5,6,7,0,1,2,3,4,5,6,7,0,1,2,3]
+WORD_CUTS = [384,512,640]
+SCALE_CUTS = [512,512,512]
+SCALE_TAGS = [0,1,0]
+BANKS = [0,1,2,3,4,5,6,7,0,1,2,3,4,5,6,7,0,1,2,3,4,5,6,7,0,1,2,3,4,5,6,7,0,1,2,3,4,5,6,7,0,1,2,3,4]
 
 
 def tile_moe_pke_glu_sigmoid_kernel(
@@ -33,9 +33,9 @@ def tile_moe_pke_glu_sigmoid_kernel(
         keep = ctx.enter_context(tc.tile_pool(name="keep", bufs=1))
         ring_gw = ctx.enter_context(tc.tile_pool(name="ring_gw", bufs=4))
         ring_sig = ctx.enter_context(tc.tile_pool(name="ring_sig", bufs=3))
-        ring_h = ctx.enter_context(tc.tile_pool(name="ring_h", bufs=3))
-        ring_ht = ctx.enter_context(tc.tile_pool(name="ring_ht", bufs=3))
-        ring_q = ctx.enter_context(tc.tile_pool(name="ring_q", bufs=4))
+        ring_h = ctx.enter_context(tc.tile_pool(name="ring_h", bufs=4))
+        ring_ht = ctx.enter_context(tc.tile_pool(name="ring_ht", bufs=4))
+        ring_q = ctx.enter_context(tc.tile_pool(name="ring_q", bufs=2))
         psum = ctx.enter_context(tc.psum_pool(name="psum", bufs=1))
 
         offsets = keep.tile([P, S // 16], U16, name="offsets")
@@ -46,14 +46,17 @@ def tile_moe_pke_glu_sigmoid_kernel(
         words = {}
         planes = {}
         for name in ("w1", "w3", "w2"):
-            words[name] = keep.tile([P, E * 1024], U8, name=name + "_words", align_bytes=64)
             planes[name] = keep.tile([P, E * 512], U8, name=name + "_plane", align_bytes=64)
         dram_words = {"w1": w1_words, "w3": w3_words, "w2": w2_words}
         dram_scales = {"w1": w1_scales, "w3": w3_scales, "w2": w2_scales}
 
         def load_words(queue, name, e0, e1):
+            if e0 == 0:
+                tag = "early" if name == "w2" else name + "_words"
+                words[name] = keep.tile([P, 2 * 1024], U8, name=tag, align_bytes=64)
+            s0 = e0 % 2
             queue.dma_start(
-                words[name][:, e0 * 1024 : e1 * 1024].bitcast(I32).rearrange("p (e w) -> p e w", e=e1 - e0),
+                words[name][:, s0 * 1024 : (s0 + e1 - e0) * 1024].bitcast(I32).rearrange("p (e w) -> p e w", e=e1 - e0),
                 dram_words[name][e0:e1, 0].rearrange("e p b -> p e b").bitcast(I32),
             )
 
@@ -74,7 +77,6 @@ def tile_moe_pke_glu_sigmoid_kernel(
         def zero(engine, name, e0, e1):
             engine.memset(planes[name][:, e0 * 512 : e1 * 512].bitcast(I32), 0)
 
-        load_xw(nc.gpsimd)
         nc.vector.memset(warm[:], 0.0)
         nc.vector.memset(xs[:], 0)
         zero(nc.vector, "w1", 0, 2)
@@ -82,16 +84,13 @@ def tile_moe_pke_glu_sigmoid_kernel(
         zero(nc.vector, "w2", 0, E)
         zero(nc.vector, "w1", 2, E)
         zero(nc.vector, "w3", 2, E)
+        load_xw(nc.scalar)
+        load_words(nc.scalar, "w1", 0, 2)
+        load_words(nc.scalar, "w3", 0, 2)
         nc.scalar.activation(warm[:], warm[:], SIGMOID)
         nc.sync.dma_start(offsets[:], offs)
         load_xs(nc.sync)
-        load_words(nc.gpsimd, "w1", 0, 2)
-        load_words(nc.gpsimd, "w3", 0, 2)
         make_identity(nc, ident[:])
-        load_words(nc.gpsimd, "w2", 0, 2)
-        load_words(nc.gpsimd, "w1", 2, E)
-        load_words(nc.gpsimd, "w3", 2, E)
-        load_words(nc.gpsimd, "w2", 2, E)
         load_scales(nc.sync, "w1", 0, 2)
         load_scales(nc.sync, "w3", 0, 2)
         load_scales(nc.sync, "w2", 0, E)
@@ -100,6 +99,7 @@ def tile_moe_pke_glu_sigmoid_kernel(
 
         gathered_words = {}
         gathered_scales = {}
+        scale_tiles = []
 
         def gather_words(g):
             s0 = sum(WORD_CUTS[:g])
@@ -116,6 +116,7 @@ def tile_moe_pke_glu_sigmoid_kernel(
             n = SCALE_CUTS[g]
             tile = keep.tile([P, n], U8, name="gs%d" % SCALE_TAGS[g], align_bytes=64)
             nc.vector.tensor_copy(tile[:], xs[:].bitcast(U8).indirect(offsets[:, s0 // 16 : (s0 + n) // 16]))
+            scale_tiles.append(tile)
             for u in range(n // P):
                 gathered_scales[s0 // P + u] = tile[:, u * P : (u + 1) * P]
 
@@ -140,15 +141,31 @@ def tile_moe_pke_glu_sigmoid_kernel(
                 acc[:],
                 lhsT=gathered_words[u].bitcast(FP8X4),
                 lhsT_scale=gathered_scales[u],
-                rhs=words[name][:, e * 1024 : (e + 1) * 1024].bitcast(FP4X4),
+                rhs=words[name][:, e % 2 * 1024 : (e % 2 + 1) * 1024].bitcast(FP4X4),
                 rhs_scale=planes[name][:, e * 512 : (e + 1) * 512],
                 start=True,
                 stop=True,
             )
             held[kind, u] = acc
 
+        def warm_up(n):
+            acc = bank("y", [P, H])
+            for k in range(n):
+                nc.tensor.matmul_mx(
+                    acc[:],
+                    lhsT=gathered_words[0].bitcast(FP8X4),
+                    lhsT_scale=gathered_scales[0],
+                    rhs=words["w1"][:, 0:1024].bitcast(FP4X4),
+                    rhs_scale=scale_tiles[0][:, 0:512],
+                    start=True,
+                    stop=True,
+                )
+
         def sigmoid(u):
-            sig = ring_sig.tile([P, H], F32, name="sig", align_bytes=64)
+            if u == 0:
+                sig = keep.tile([P, H], F32, name="early", align_bytes=64)
+            else:
+                sig = ring_sig.tile([P, H], F32, name="sig", align_bytes=64)
             nc.scalar.activation(
                 sig[:].rearrange("s (v p d) -> s v p d", v=2, d=2),
                 held["a", u][:].rearrange("s (p v d) -> s v p d", v=2, d=2),
@@ -193,7 +210,7 @@ def tile_moe_pke_glu_sigmoid_kernel(
             for k, t in enumerate(ts):
                 nc.tensor.matmul_mx(
                     y[:, k, :],
-                    lhsT=words["w2"][:, e * 1024 + t * 256 : e * 1024 + (t + 1) * 256].bitcast(FP4X4),
+                    lhsT=words["w2"][:, e % 2 * 1024 + t * 256 : e % 2 * 1024 + (t + 1) * 256].bitcast(FP4X4),
                     lhsT_scale=planes["w2"][:, e * 512 + t * P : e * 512 + (t + 1) * P],
                     rhs=codes[:].bitcast(FP8X4),
                     rhs_scale=scales[:],
@@ -219,125 +236,130 @@ def tile_moe_pke_glu_sigmoid_kernel(
 
         gather_scales(0)
         gather_words(0)
-        gather_scales(1)
-        first("a", 0)
-        first("a", 1)
-        first("b", 0)
-        sigmoid(0)
-        gate(0)
+        warm_up(3)
         gather_words(1)
-        first("a", 2)
+        first("a", 0)
+        first("b", 0)
+        first("a", 1)
+        load_words(nc.sync, "w1", 2, 3)
+        sigmoid(0)
         first("b", 1)
+        load_words(nc.sync, "w3", 2, 3)
+        first("a", 2)
         sigmoid(1)
-        gate(1)
-        first("a", 3)
+        gate(0)
+        load_words(nc.sync, "w2", 0, 2)
         first("b", 2)
+        gather_scales(1)
+        first("a", 3)
+        load_words(nc.sync, "w1", 3, 4)
         sigmoid(2)
-        gate(2)
-        first("a", 4)
+        gate(1)
         first("b", 3)
-        sigmoid(3)
-        gate(3)
+        load_words(nc.sync, "w3", 3, 4)
         turn([0,1])
-        first("a", 5)
+        first("a", 4)
+        sigmoid(3)
+        gate(2)
         first("b", 4)
+        first("a", 5)
+        load_words(nc.sync, "w1", 4, 5)
         sigmoid(4)
+        gate(3)
+        first("b", 5)
+        load_words(nc.sync, "w3", 4, 5)
+        gather_words(2)
+        turn([2,3])
         collect([0,1], "A")
         quantise([0,1])
-        gather_scales(2)
-        gate(4)
-        first("a", 6)
-        first("b", 5)
-        sigmoid(5)
-        gather_words(2)
-        gate(5)
-        turn([2,3])
-        second([0,1], [0,1])
-        first("a", 7)
-        first("b", 6)
-        sigmoid(6)
         collect([2,3], "A")
-        quantise([2,3])
+        gather_scales(2)
+        first("a", 6)
+        sigmoid(5)
+        gate(4)
+        second([0,1], [0,1])
         second([0,1], [2,3])
-        gate(6)
-        empty([0,1], [0,1], "V")
-        first("a", 8)
-        first("b", 7)
-        sigmoid(7)
-        empty([0,1], [2,3], "A")
-        gather_scales(3)
-        gate(7)
+        load_words(nc.sync, "w2", 2, 3)
+        first("b", 6)
+        quantise([2,3])
+        first("a", 7)
+        load_words(nc.sync, "w1", 5, 6)
+        sigmoid(6)
+        gate(5)
         turn([4,5])
+        first("b", 7)
+        load_words(nc.sync, "w3", 5, 6)
         second([2,3], [0,1])
+        collect([4,5], "V")
+        empty([0,1], [0,1], "A")
+        empty([0,1], [2,3], "V")
+        quantise([4,5])
+        first("a", 8)
+        sigmoid(7)
+        gate(6)
+        first("b", 8)
+        second([2,3], [2,3])
+        load_words(nc.sync, "w2", 3, 4)
         empty([2,3], [0,1], "A")
         store(nc.sync, 0, 1, 0, 4, 0, 2)
         store(nc.sync, 1, 2, 0, 4, 0, 2)
         first("a", 9)
-        first("b", 8)
         sigmoid(8)
-        collect([4,5], "V")
-        quantise([4,5])
-        second([2,3], [2,3])
-        empty([2,3], [2,3], "A")
+        gate(7)
+        first("b", 9)
+        first("a", 10)
+        sigmoid(9)
+        gate(8)
+        first("b", 10)
+        empty([2,3], [2,3], "V")
         store(nc.sync, 2, 3, 0, 4, 0, 2)
         store(nc.sync, 3, 4, 0, 4, 0, 2)
-        gate(8)
         turn([6,7])
-        first("a", 10)
-        first("b", 9)
-        sigmoid(9)
-        collect([6,7], "V")
-        gate(9)
-        quantise([6,7])
-        second([4,5], [0,1])
         first("a", 11)
-        first("b", 10)
         sigmoid(10)
-        second([4,5], [2,3])
-        gate(10)
-        empty([4,5], [0,1], "A")
-        store(nc.sync, 0, 1, 0, 4, 2, 3)
-        store(nc.sync, 1, 2, 0, 4, 2, 3)
+        gate(9)
+        collect([6,7], "A")
+        quantise([6,7])
         first("b", 11)
-        sigmoid(11)
         turn([8,9])
-        second([6,7], [0,1])
-        empty([4,5], [2,3], "V")
-        store(nc.sync, 2, 3, 0, 4, 2, 3)
-        store(nc.sync, 3, 4, 0, 4, 2, 3)
+        second([4,5], [0,1])
+        sigmoid(11)
+        gate(10)
+        second([4,5], [2,3])
+        load_words(nc.sync, "w2", 4, 5)
         gate(11)
+        second([6,7], [0,1])
+        empty([4,5], [0,1], "V")
         collect([8,9], "A")
         second([6,7], [2,3])
+        load_words(nc.sync, "w2", 5, 6)
         turn([10])
-        quantise([8,9])
-        empty([6,7], [0,1], "A")
-        store(nc.sync, 0, 1, 0, 4, 3, 4)
-        store(nc.sync, 1, 2, 0, 4, 3, 4)
         turn([11])
-        collect([10], "V")
-        empty([6,7], [2,3], "A")
-        store(nc.sync, 2, 3, 0, 4, 3, 4)
-        store(nc.sync, 3, 4, 0, 4, 3, 4)
+        quantise([8,9])
+        empty([4,5], [2,3], "V")
         collect([11], "A")
+        empty([6,7], [0,1], "A")
+        store(nc.sync, 0, 1, 0, 4, 2, 4)
+        store(nc.sync, 1, 2, 0, 4, 2, 4)
         quantise([11])
-        quantise([10])
-        second([11], [0,1])
+        empty([6,7], [2,3], "A")
+        store(nc.sync, 2, 3, 0, 4, 2, 4)
+        store(nc.sync, 3, 4, 0, 4, 2, 4)
+        collect([10], "V")
         second([8,9], [0,1])
-        second([10], [0,1,2,3])
-        second([11], [2,3])
+        second([11], [0,1])
+        empty([8,9], [0,1], "A")
         second([8,9], [2,3])
         empty([11], [0,1], "A")
-        store(nc.sync, 0, 2, 2, 3, 5, 6)
-        store(nc.sync, 0, 2, 3, 4, 5, 6)
-        empty([8,9], [0,1], "V")
-        empty([10], [0,1,2,3], "V")
-        empty([11], [2,3], "V")
-        store(nc.sync, 0, 1, 0, 4, 4, 5)
-        store(nc.sync, 1, 2, 0, 4, 4, 5)
-        store(nc.sync, 0, 4, 0, 1, 5, 6)
-        store(nc.sync, 0, 4, 1, 2, 5, 6)
-        store(nc.sync, 2, 4, 2, 3, 5, 6)
-        store(nc.sync, 2, 4, 3, 4, 5, 6)
+        store(nc.sync, 0, 2, 2, 3, 4, 6)
+        store(nc.sync, 0, 2, 3, 4, 4, 6)
+        quantise([10])
+        second([11], [2,3])
         empty([8,9], [2,3], "A")
-        store(nc.sync, 2, 3, 0, 4, 4, 5)
-        store(nc.sync, 3, 4, 0, 4, 4, 5)
+        empty([11], [2,3], "V")
+        store(nc.sync, 2, 4, 2, 3, 4, 6)
+        store(nc.sync, 2, 4, 3, 4, 4, 6)
+        second([10], [0,1,2,3])
+        empty([10], [0,1,2,3], "V")
+        store(nc.sync, 0, 4, 0, 1, 4, 6)
+        store(nc.sync, 0, 4, 1, 2, 4, 6)

@@ -19,10 +19,30 @@ SIGMOID = mybir.ActivationFunctionType.Sigmoid
 MULT = mybir.AluOpType.mult
 
 P = 128
-WORD_CUTS = [384,512,640]
-SCALE_CUTS = [512,512,512]
-SCALE_TAGS = [0,1,0]
-BANKS = [0,1,2,3,4,5,6,7,0,1,2,3,4,5,6,7,0,1,2,3,4,5,6,7,0,1,2,3,4,5,6,7,0,1,2,3,4,5,6,7,0,1,2,3,4]
+UNITS = S // P
+WORD_CUT = 384
+SCALE_CUT = S
+LATER = (("w1", 2, 4), ("w3", 2, 4), ("w2", 0, 2), ("w1", 4, 6), ("w3", 4, 6), ("w2", 2, 6))
+SLOTS = {"w1": 2, "w3": 2}
+TB = 1
+YB = 2
+LAST = [(10,), (11,)]
+LEAD_A = 1.5
+LEAD_B = 1.3
+LAG_G = 0.6
+LAG_T = 0.55
+LAG_C = 0.95
+LAG_Q = 1.55
+LAG_Y = 2.65
+LAG_E0 = 3.2
+LAG_E1 = 3.9
+COLLECT = "AAAAAA"
+EMPTY0 = "VVVVVV"
+EMPTY1 = "AAAAAA"
+W3 = 3.3
+S2 = 4.5
+QUADRANTS = (0, 2, 1, 3)
+ORDER = [0, 2, 1, 3, 4, 6, 5, 7, 8, 10, 9, 11]
 
 
 def tile_moe_pke_glu_sigmoid_kernel(
@@ -31,79 +51,68 @@ def tile_moe_pke_glu_sigmoid_kernel(
     nc = tc.nc
     with ExitStack() as ctx:
         keep = ctx.enter_context(tc.tile_pool(name="keep", bufs=1))
-        ring_gw = ctx.enter_context(tc.tile_pool(name="ring_gw", bufs=4))
-        ring_sig = ctx.enter_context(tc.tile_pool(name="ring_sig", bufs=3))
+        ring_gw = ctx.enter_context(tc.tile_pool(name="ring_gw", bufs=3))
+        ring_gs = ctx.enter_context(tc.tile_pool(name="ring_gs", bufs=2))
+        ring_sig = ctx.enter_context(tc.tile_pool(name="ring_sig", bufs=4))
         ring_h = ctx.enter_context(tc.tile_pool(name="ring_h", bufs=4))
-        ring_ht = ctx.enter_context(tc.tile_pool(name="ring_ht", bufs=4))
+        ring_ht = ctx.enter_context(tc.tile_pool(name="ring_ht", bufs=2))
         ring_q = ctx.enter_context(tc.tile_pool(name="ring_q", bufs=2))
-        psum = ctx.enter_context(tc.psum_pool(name="psum", bufs=1))
+        psum = ctx.enter_context(tc.psum_pool(name="psum", bufs=2))
 
         offsets = keep.tile([P, S // 16], U16, name="offsets")
-        xw = keep.tile([P, T], I32, name="xw", align_bytes=64)
-        xs = keep.tile([P, T // 4], I32, name="xs", align_bytes=64)
+        xs = keep.tile([P, T // 4], I32, name="xs", tag="xs", align_bytes=64)
         ident = keep.tile([P, P], F32, name="ident", align_bytes=64)
-        warm = keep.tile([P, 1], F32, name="warm")
-        words = {}
-        planes = {}
-        for name in ("w1", "w3", "w2"):
-            planes[name] = keep.tile([P, E * 512], U8, name=name + "_plane", align_bytes=64)
         dram_words = {"w1": w1_words, "w3": w3_words, "w2": w2_words}
         dram_scales = {"w1": w1_scales, "w3": w3_scales, "w2": w2_scales}
+        words = {}
+        planes = {}
 
-        def load_words(queue, name, e0, e1):
-            if e0 == 0:
-                tag = "early" if name == "w2" else name + "_words"
-                words[name] = keep.tile([P, 2 * 1024], U8, name=tag, align_bytes=64)
-            s0 = e0 % 2
+        def load_words(queue, name, tile, slot, e0, e1):
+            part = tile[:, slot * 1024 : (slot + e1 - e0) * 1024]
             queue.dma_start(
-                words[name][:, s0 * 1024 : (s0 + e1 - e0) * 1024].bitcast(I32).rearrange("p (e w) -> p e w", e=e1 - e0),
+                part.bitcast(I32).rearrange("p (e w) -> p e w", e=e1 - e0),
                 dram_words[name][e0:e1, 0].rearrange("e p b -> p e b").bitcast(I32),
             )
+            for e in range(e0, e1):
+                words[name, e] = part[:, (e - e0) * 1024 : (e - e0 + 1) * 1024]
 
-        def load_scales(queue, name, e0, e1):
-            for j in range(4):
-                queue.dma_start(
-                    planes[name][j:P:32, e0 * 512 : e1 * 512].bitcast(I32).rearrange("p (e w) -> p e w", e=e1 - e0),
-                    dram_scales[name][e0:e1, 0, j:16:4, :].rearrange("e q b -> q e b").bitcast(I32),
+        def load_scales(queues, name, tile, e0, e1):
+            for j, q in enumerate(QUADRANTS):
+                queues[j].dma_start(
+                    tile[32 * q : 32 * q + 4, : (e1 - e0) * 512].bitcast(I32).rearrange("p (e w) -> p e w", e=e1 - e0),
+                    dram_scales[name][e0:e1, 0, 4 * q : 4 * q + 4, :].rearrange("e q b -> q e b").bitcast(I32),
                 )
+            for e in range(e0, e1):
+                planes[name, e] = tile[:, (e - e0) * 512 : (e - e0 + 1) * 512]
 
-        def load_xs(queue):
-            for j in range(4):
-                queue.dma_start(xs[j:P:32, :], x_scales[0, j:16:4, :].bitcast(I32))
+        def zeroed_plane(name, experts):
+            tile = keep.tile([P, experts * 512], U8, name=name + "_plane", align_bytes=64)
+            nc.vector.memset(tile[:].bitcast(I32), 0)
+            return tile
 
-        def load_xw(queue):
-            queue.dma_start(xw[:], x_words[0].rearrange("p t r -> p (t r)").bitcast(I32))
-
-        def zero(engine, name, e0, e1):
-            engine.memset(planes[name][:, e0 * 512 : e1 * 512].bitcast(I32), 0)
-
-        nc.vector.memset(warm[:], 0.0)
-        nc.vector.memset(xs[:], 0)
-        zero(nc.vector, "w1", 0, 2)
-        zero(nc.vector, "w3", 0, 2)
-        zero(nc.vector, "w2", 0, E)
-        zero(nc.vector, "w1", 2, E)
-        zero(nc.vector, "w3", 2, E)
-        load_xw(nc.scalar)
-        load_words(nc.scalar, "w1", 0, 2)
-        load_words(nc.scalar, "w3", 0, 2)
-        nc.scalar.activation(warm[:], warm[:], SIGMOID)
+        sync, scalar = nc.sync, nc.scalar
         nc.sync.dma_start(offsets[:], offs)
-        load_xs(nc.sync)
+        early = {}
+        for name in ("w1", "w3"):
+            early[name] = keep.tile([P, 2 * 1024], U8, name=name + "_words", align_bytes=64)
+        load_words(scalar, "w1", early["w1"], 0, 0, 2)
+        load_words(scalar, "w3", early["w3"], 0, 0, 1)
+        nc.vector.memset(xs[:], 0)
+        for queue, q in zip((sync, scalar, sync, sync), QUADRANTS):
+            queue.dma_start(xs[32 * q : 32 * q + 4, :], x_scales[0, 4 * q : 4 * q + 4, :].bitcast(I32))
+        load_words(scalar, "w3", early["w3"], 1, 1, 2)
+        xw = keep.tile([P, T], I32, name="xw", align_bytes=64)
+        scalar.dma_start(xw[:], x_words[0].rearrange("p t r -> p (t r)").bitcast(I32))
         make_identity(nc, ident[:])
-        load_scales(nc.sync, "w1", 0, 2)
-        load_scales(nc.sync, "w3", 0, 2)
-        load_scales(nc.sync, "w2", 0, E)
-        load_scales(nc.sync, "w1", 2, E)
-        load_scales(nc.sync, "w3", 2, E)
+        plane = {name: zeroed_plane(name, E) for name in ("w1", "w3", "w2")}
+        load_scales([sync] * 4, "w1", plane["w1"], 0, E)
+        load_scales([scalar] * 3 + [sync], "w3", plane["w3"], 0, E)
 
         gathered_words = {}
         gathered_scales = {}
-        scale_tiles = []
 
         def gather_words(g):
-            s0 = sum(WORD_CUTS[:g])
-            n = WORD_CUTS[g]
+            s0, n = g * WORD_CUT, WORD_CUT
             tile = ring_gw.tile([P, n], I32, name="gw", align_bytes=64)
             nc.vector.tensor_copy(
                 tile[:].bitcast(U32), xw[:].bitcast(U32).indirect(offsets[:, s0 // 16 : (s0 + n) // 16])
@@ -112,20 +121,13 @@ def tile_moe_pke_glu_sigmoid_kernel(
                 gathered_words[s0 // P + u] = tile[:, u * P : (u + 1) * P]
 
         def gather_scales(g):
-            s0 = sum(SCALE_CUTS[:g])
-            n = SCALE_CUTS[g]
-            tile = keep.tile([P, n], U8, name="gs%d" % SCALE_TAGS[g], align_bytes=64)
+            s0, n = g * SCALE_CUT, SCALE_CUT
+            tile = ring_gs.tile([P, n], U8, name="gs", align_bytes=64)
             nc.vector.tensor_copy(tile[:], xs[:].bitcast(U8).indirect(offsets[:, s0 // 16 : (s0 + n) // 16]))
-            scale_tiles.append(tile)
             for u in range(n // P):
                 gathered_scales[s0 // P + u] = tile[:, u * P : (u + 1) * P]
 
         held = {}
-        taken = []
-
-        def bank(kind, shape):
-            taken.append(kind)
-            return psum.tile(shape, F32, name="bank%d" % BANKS[len(taken) - 1])
 
         def copy(engine, dst, src):
             if engine == "V":
@@ -133,233 +135,144 @@ def tile_moe_pke_glu_sigmoid_kernel(
             else:
                 nc.scalar.copy(dst, src)
 
-        def first(kind, u):
+        def first(kind, k):
+            if k >= UNITS:
+                return
+            u = ORDER[k]
             e = u // 2
             name = {"a": "w1", "b": "w3"}[kind]
-            acc = bank(kind, [P, H])
+            acc = psum.tile([P, H], F32, name=kind, bufs={"a": 2, "b": 3}[kind])
             nc.tensor.matmul_mx(
                 acc[:],
                 lhsT=gathered_words[u].bitcast(FP8X4),
                 lhsT_scale=gathered_scales[u],
-                rhs=words[name][:, e % 2 * 1024 : (e % 2 + 1) * 1024].bitcast(FP4X4),
-                rhs_scale=planes[name][:, e * 512 : (e + 1) * 512],
+                rhs=words[name, e].bitcast(FP4X4),
+                rhs_scale=planes[name, e],
                 start=True,
                 stop=True,
             )
-            held[kind, u] = acc
+            held[kind, k] = acc
 
-        def warm_up(n):
-            acc = bank("y", [P, H])
-            for k in range(n):
-                nc.tensor.matmul_mx(
-                    acc[:],
-                    lhsT=gathered_words[0].bitcast(FP8X4),
-                    lhsT_scale=gathered_scales[0],
-                    rhs=words["w1"][:, 0:1024].bitcast(FP4X4),
-                    rhs_scale=scale_tiles[0][:, 0:512],
-                    start=True,
-                    stop=True,
-                )
-
-        def sigmoid(u):
-            if u == 0:
-                sig = keep.tile([P, H], F32, name="early", align_bytes=64)
-            else:
-                sig = ring_sig.tile([P, H], F32, name="sig", align_bytes=64)
+        def sigmoid(k):
+            if k >= UNITS:
+                return
+            sig = ring_sig.tile([P, H], F32, name="sig", align_bytes=64)
             nc.scalar.activation(
                 sig[:].rearrange("s (v p d) -> s v p d", v=2, d=2),
-                held["a", u][:].rearrange("s (p v d) -> s v p d", v=2, d=2),
+                held["a", k][:].rearrange("s (p v d) -> s v p d", v=2, d=2),
                 SIGMOID,
             )
-            held["sig", u] = sig
+            held["sig", k] = sig
 
-        def gate(u):
+        def gate(k):
+            if not 0 <= k < UNITS:
+                return
             h = ring_h.tile([P, H], BF16, name="h", align_bytes=64)
             nc.vector.tensor_tensor(
                 h[:].rearrange("s (v p d) -> s v p d", v=2, d=2),
-                held["b", u][:].rearrange("s (p v d) -> s v p d", v=2, d=2),
-                held["sig", u][:].rearrange("s (v p d) -> s v p d", v=2, d=2),
+                held["b", k][:].rearrange("s (p v d) -> s v p d", v=2, d=2),
+                held["sig", k][:].rearrange("s (v p d) -> s v p d", v=2, d=2),
                 MULT,
             )
-            held["h", u] = h
+            held["h", k] = h
 
-        def turn(us):
-            turned = bank("t", [P, len(us), 2, P])
-            for half, u in enumerate(us):
-                pairs = held["h", u][:].bitcast(F32)
+        def turn(ks):
+            turned = psum.tile([P, len(ks), 2, P], F32, name="t", bufs=TB)
+            for half in reversed(range(len(ks))):
+                pairs = held["h", ks[half]][:].bitcast(F32)
                 for v in range(2):
                     nc.tensor.transpose(turned[:, half, v, :], pairs[:, v * P : (v + 1) * P], ident[:])
-            held["t", us[0]] = turned
+            held["t", ks] = turned
 
-        def collect(us, engine):
-            ht = ring_ht.tile([P, 4 * P * len(us)], BF16, name="ht", align_bytes=64)
-            dst = ht[:].bitcast(F32).rearrange("p (a s v) -> p a s v", a=len(us), v=2)
-            copy(engine, dst, held["t", us[0]][:].rearrange("p a v s -> p a s v"))
-            held["ht", us[0]] = ht
+        def collect(ks, engine):
+            ht = ring_ht.tile([P, 4 * P * len(ks)], BF16, name="ht", align_bytes=64)
+            dst = ht[:].bitcast(F32).rearrange("p (a s v) -> p a s v", a=len(ks), v=2)
+            copy(engine, dst, held["t", ks][:].rearrange("p a v s -> p a s v"))
+            held["ht", ks] = ht
 
-        def quantise(us):
-            codes = ring_q.tile([P, P * len(us)], U32, name="codes", align_bytes=64)
-            scales = ring_q.tile([P, P * len(us)], U8, name="scales", align_bytes=64)
-            nc.vector.quantize_mx(codes[:].bitcast(FP8X4), scales[:], held["ht", us[0]][:])
-            held["q", us[0]] = (codes, scales)
+        def quantise(ks):
+            codes = ring_q.tile([P, P * len(ks)], U32, name="codes", align_bytes=64)
+            scales = ring_q.tile([P, P * len(ks)], U8, name="scales", align_bytes=64)
+            nc.vector.quantize_mx(codes[:].bitcast(FP8X4), scales[:], held["ht", ks][:])
+            held["q", ks] = (codes, scales)
 
-        def second(us, ts):
-            e = us[0] // 2
-            codes, scales = held["q", us[0]]
-            y = bank("y", [P, len(ts), P * len(us)])
-            for k, t in enumerate(ts):
-                nc.tensor.matmul_mx(
-                    y[:, k, :],
-                    lhsT=words["w2"][:, e % 2 * 1024 + t * 256 : e % 2 * 1024 + (t + 1) * 256].bitcast(FP4X4),
-                    lhsT_scale=planes["w2"][:, e * 512 + t * P : e * 512 + (t + 1) * P],
-                    rhs=codes[:].bitcast(FP8X4),
-                    rhs_scale=scales[:],
-                    start=True,
-                    stop=True,
-                )
-            held["y", us[0], ts[0]] = y
+        def one_expert(g):
+            return ORDER[2 * g] // 2 == ORDER[2 * g + 1] // 2
+
+        def second(ks):
+            codes, scales = held["q", ks]
+            g = ks[0] // 2
+            n = 2 * P if one_expert(g) and len(ks) == 2 else P
+            for half in range(2):
+                if ks[0] % 2 == 0:
+                    held["y", g, half] = psum.tile([P, 2, 2 * P], F32, name="y", bufs=YB)
+                y = held["y", g, half]
+                for j in range(2):
+                    t = 2 * half + j
+                    for c0 in range(0, P * len(ks), n):
+                        k = ks[c0 // P]
+                        e = ORDER[k] // 2
+                        nc.tensor.matmul_mx(
+                            y[:, j, k % 2 * P : k % 2 * P + n],
+                            lhsT=words["w2", e][:, t * 256 : (t + 1) * 256].bitcast(FP4X4),
+                            lhsT_scale=planes["w2", e][:, t * P : (t + 1) * P],
+                            rhs=codes[:, c0 : c0 + n].bitcast(FP8X4),
+                            rhs_scale=scales[:, c0 : c0 + n],
+                            start=True,
+                            stop=True,
+                        )
 
         result = keep.tile([P, 4, R, E * 64], F32, name="result", align_bytes=64)
         rows = out.rearrange("(t p) (m c) -> p t m c", p=P, m=R)
 
-        def empty(us, ts, engine):
-            e = us[0] // 2
-            m0 = 2 * (us[0] % 2)
-            dst = result[:, ts[0] : ts[-1] + 1, m0 : m0 + 2 * len(us), 64 * e : 64 * e + 64]
-            copy(engine, dst, held["y", us[0], ts[0]][:].rearrange("p k (m c) -> p k m c", c=64))
-
-        def store(queue, t0, t1, m0, m1, e0, e1):
-            if t1 - t0 == 1:
-                queue.dma_start(rows[:, t0, m0:m1, 64 * e0 : 64 * e1], result[:, t0, m0:m1, 64 * e0 : 64 * e1])
+        def empty(g, half, engine):
+            ts = (2 * half, 2 * half + 1)
+            u = ORDER[2 * g]
+            e = u // 2
+            if one_expert(g):
+                src = held["y", g, half][:].rearrange("p k (m c) -> p k m c", c=64)
+                copy(engine, result[:, ts[0] : ts[1] + 1, :, 64 * e : 64 * e + 64], src)
+                if e % 2 == 1:
+                    cols = slice(64 * (e - 1), 64 * (e + 1))
+                    for t in ts:
+                        nc.sync.dma_start(rows[:, t, :, cols], result[:, t, :, cols])
             else:
-                queue.dma_start(rows[:, t0:t1, m0, 64 * e0 : 64 * e1], result[:, t0:t1, m0, 64 * e0 : 64 * e1])
+                ms = slice(2 * (u % 2), 2 * (u % 2) + 2)
+                cols = slice(64 * e, 64 * (e + 2))
+                src = held["y", g, half][:].rearrange("p k (e m c) -> p k m e c", e=2, c=64)
+                dst = result[:, ts[0] : ts[1] + 1, ms, cols].rearrange("p k m (e c) -> p k m e c", e=2)
+                copy(engine, dst, src)
+                for t in ts:
+                    nc.sync.dma_start(rows[:, t, ms, cols], result[:, t, ms, cols])
 
+        G = UNITS // 2
+        parts = [(2 * g, 2 * g + 1) for g in range(G - 1)] + LAST
+        calls = []
+        for k in range(UNITS):
+            calls.append((k - LEAD_A, first, ("a", k)))
+            calls.append((k, sigmoid, (k,)))
+            calls.append((k + LAG_G - LEAD_B, first, ("b", k)))
+            calls.append((k + LAG_G, gate, (k,)))
+        for ks in parts:
+            k = ks[-1] + LAG_G
+            g = ks[0] // 2
+            calls.append((k + LAG_T, turn, (ks,)))
+            calls.append((k + LAG_C, collect, (ks, COLLECT[g])))
+            calls.append((k + LAG_Q, quantise, (ks,)))
+            calls.append((k + LAG_Y, second, (ks,)))
+            if ks[-1] % 2 == 1:
+                calls.append((k + LAG_E0, empty, (g, 0, EMPTY0[g])))
+                calls.append((k + LAG_E1, empty, (g, 1, EMPTY1[g])))
+        calls.append((W3, gather_words, (3,)))
         gather_scales(0)
-        gather_words(0)
-        warm_up(3)
-        gather_words(1)
-        first("a", 0)
-        first("b", 0)
-        first("a", 1)
-        load_words(nc.sync, "w1", 2, 3)
-        sigmoid(0)
-        first("b", 1)
-        load_words(nc.sync, "w3", 2, 3)
-        first("a", 2)
-        sigmoid(1)
-        gate(0)
-        load_words(nc.sync, "w2", 0, 2)
-        first("b", 2)
-        gather_scales(1)
-        first("a", 3)
-        load_words(nc.sync, "w1", 3, 4)
-        sigmoid(2)
-        gate(1)
-        first("b", 3)
-        load_words(nc.sync, "w3", 3, 4)
-        turn([0,1])
-        first("a", 4)
-        sigmoid(3)
-        gate(2)
-        first("b", 4)
-        first("a", 5)
-        load_words(nc.sync, "w1", 4, 5)
-        sigmoid(4)
-        gate(3)
-        first("b", 5)
-        load_words(nc.sync, "w3", 4, 5)
-        gather_words(2)
-        turn([2,3])
-        collect([0,1], "A")
-        quantise([0,1])
-        collect([2,3], "A")
-        gather_scales(2)
-        first("a", 6)
-        sigmoid(5)
-        gate(4)
-        second([0,1], [0,1])
-        second([0,1], [2,3])
-        load_words(nc.sync, "w2", 2, 3)
-        first("b", 6)
-        quantise([2,3])
-        first("a", 7)
-        load_words(nc.sync, "w1", 5, 6)
-        sigmoid(6)
-        gate(5)
-        turn([4,5])
-        first("b", 7)
-        load_words(nc.sync, "w3", 5, 6)
-        second([2,3], [0,1])
-        collect([4,5], "V")
-        empty([0,1], [0,1], "A")
-        empty([0,1], [2,3], "V")
-        quantise([4,5])
-        first("a", 8)
-        sigmoid(7)
-        gate(6)
-        first("b", 8)
-        second([2,3], [2,3])
-        load_words(nc.sync, "w2", 3, 4)
-        empty([2,3], [0,1], "A")
-        store(nc.sync, 0, 1, 0, 4, 0, 2)
-        store(nc.sync, 1, 2, 0, 4, 0, 2)
-        first("a", 9)
-        sigmoid(8)
-        gate(7)
-        first("b", 9)
-        first("a", 10)
-        sigmoid(9)
-        gate(8)
-        first("b", 10)
-        empty([2,3], [2,3], "V")
-        store(nc.sync, 2, 3, 0, 4, 0, 2)
-        store(nc.sync, 3, 4, 0, 4, 0, 2)
-        turn([6,7])
-        first("a", 11)
-        sigmoid(10)
-        gate(9)
-        collect([6,7], "A")
-        quantise([6,7])
-        first("b", 11)
-        turn([8,9])
-        second([4,5], [0,1])
-        sigmoid(11)
-        gate(10)
-        second([4,5], [2,3])
-        load_words(nc.sync, "w2", 4, 5)
-        gate(11)
-        second([6,7], [0,1])
-        empty([4,5], [0,1], "V")
-        collect([8,9], "A")
-        second([6,7], [2,3])
-        load_words(nc.sync, "w2", 5, 6)
-        turn([10])
-        turn([11])
-        quantise([8,9])
-        empty([4,5], [2,3], "V")
-        collect([11], "A")
-        empty([6,7], [0,1], "A")
-        store(nc.sync, 0, 1, 0, 4, 2, 4)
-        store(nc.sync, 1, 2, 0, 4, 2, 4)
-        quantise([11])
-        empty([6,7], [2,3], "A")
-        store(nc.sync, 2, 3, 0, 4, 2, 4)
-        store(nc.sync, 3, 4, 0, 4, 2, 4)
-        collect([10], "V")
-        second([8,9], [0,1])
-        second([11], [0,1])
-        empty([8,9], [0,1], "A")
-        second([8,9], [2,3])
-        empty([11], [0,1], "A")
-        store(nc.sync, 0, 2, 2, 3, 4, 6)
-        store(nc.sync, 0, 2, 3, 4, 4, 6)
-        quantise([10])
-        second([11], [2,3])
-        empty([8,9], [2,3], "A")
-        empty([11], [2,3], "V")
-        store(nc.sync, 2, 4, 2, 3, 4, 6)
-        store(nc.sync, 2, 4, 3, 4, 4, 6)
-        second([10], [0,1,2,3])
-        empty([10], [0,1,2,3], "V")
-        store(nc.sync, 0, 4, 0, 1, 4, 6)
-        store(nc.sync, 0, 4, 1, 2, 4, 6)
+        later = keep.tile([P, 14 * 1024], U8, name="later_words", tag="xs", align_bytes=64)
+        slot = 0
+        for name, e0, e1 in LATER:
+            load_words(sync, name, later, slot, e0, e1)
+            slot = slot + e1 - e0
+            if (name, e0) == ("w2", 0):
+                load_scales([scalar, scalar, sync, sync], "w2", plane["w2"], 0, E)
+        for c in range(3):
+            gather_words(c)
+        for when, call, args in sorted(calls, key=lambda c: c[0]):
+            call(*args)

@@ -21,29 +21,14 @@ MULT = mybir.AluOpType.mult
 P = 128
 UNITS = S // P
 WORD_CUT = 384
-SCALE_CUT = S
+WORD_TAGS = (0, 1, 2, 1)
+SCALE_CUTS = (640, 384, 512)
+SCALE_TAGS = (0, 1, 0)
 LATER = (("w1", 2, 4), ("w3", 2, 4), ("w2", 0, 2), ("w1", 4, 6), ("w3", 4, 6), ("w2", 2, 6))
-SLOTS = {"w1": 2, "w3": 2}
-TB = 1
-YB = 2
-LAST = [(10,), (11,)]
-LEAD_A = 1.5
-LEAD_B = 1.3
-LAG_G = 0.6
-LAG_T = 0.55
-LAG_C = 0.95
-LAG_Q = 1.55
-LAG_Y = 2.65
-LAG_E0 = 3.2
-LAG_E1 = 3.9
-COLLECT = "AAAAAA"
-EMPTY0 = "VVVVVV"
-EMPTY1 = "AAAAAA"
-W3 = 3.3
-S2 = 4.5
+BANKS = {"a": 2, "b": 3, "t": 1, "y": 2}
+EMPTY0 = "AVVVVV"
 QUADRANTS = (0, 2, 1, 3)
-ORDER = [0, 2, 1, 3, 4, 6, 5, 7, 8, 10, 9, 11]
-
+ORDER = [0, 1, 2, 3, 4, 6, 5, 7, 8, 10, 9, 11]
 
 def tile_moe_pke_glu_sigmoid_kernel(
     tc, x_words, x_scales, w1_words, w1_scales, w3_words, w3_scales, w2_words, w2_scales, offs, out
@@ -51,8 +36,6 @@ def tile_moe_pke_glu_sigmoid_kernel(
     nc = tc.nc
     with ExitStack() as ctx:
         keep = ctx.enter_context(tc.tile_pool(name="keep", bufs=1))
-        ring_gw = ctx.enter_context(tc.tile_pool(name="ring_gw", bufs=3))
-        ring_gs = ctx.enter_context(tc.tile_pool(name="ring_gs", bufs=2))
         ring_sig = ctx.enter_context(tc.tile_pool(name="ring_sig", bufs=4))
         ring_h = ctx.enter_context(tc.tile_pool(name="ring_h", bufs=4))
         ring_ht = ctx.enter_context(tc.tile_pool(name="ring_ht", bufs=2))
@@ -60,7 +43,7 @@ def tile_moe_pke_glu_sigmoid_kernel(
         psum = ctx.enter_context(tc.psum_pool(name="psum", bufs=2))
 
         offsets = keep.tile([P, S // 16], U16, name="offsets")
-        xs = keep.tile([P, T // 4], I32, name="xs", tag="xs", align_bytes=64)
+        xs = keep.tile([P, T // 4], I32, name="xs", align_bytes=64)
         ident = keep.tile([P, P], F32, name="ident", align_bytes=64)
         dram_words = {"w1": w1_words, "w3": w3_words, "w2": w2_words}
         dram_scales = {"w1": w1_scales, "w3": w3_scales, "w2": w2_scales}
@@ -92,28 +75,35 @@ def tile_moe_pke_glu_sigmoid_kernel(
 
         sync, scalar = nc.sync, nc.scalar
         nc.sync.dma_start(offsets[:], offs)
-        early = {}
-        for name in ("w1", "w3"):
-            early[name] = keep.tile([P, 2 * 1024], U8, name=name + "_words", align_bytes=64)
-        load_words(scalar, "w1", early["w1"], 0, 0, 2)
-        load_words(scalar, "w3", early["w3"], 0, 0, 1)
+
+        def word_tile(name, e0, e1):
+            return keep.tile([P, (e1 - e0) * 1024], U8, name="%s_words%d" % (name, e0), align_bytes=64)
+
+        load_words(scalar, "w1", word_tile("w1", 0, 2), 0, 0, 2)
+        load_words(sync, "w3", word_tile("w3", 0, 2), 0, 0, 2)
         nc.vector.memset(xs[:], 0)
-        for queue, q in zip((sync, scalar, sync, sync), QUADRANTS):
+        warm = keep.tile([P, 1], F32, name="warm")
+        nc.vector.memset(warm[:], 0.0)
+        for queue, q in zip((scalar, sync, scalar, sync), QUADRANTS):
             queue.dma_start(xs[32 * q : 32 * q + 4, :], x_scales[0, 4 * q : 4 * q + 4, :].bitcast(I32))
-        load_words(scalar, "w3", early["w3"], 1, 1, 2)
         xw = keep.tile([P, T], I32, name="xw", align_bytes=64)
-        scalar.dma_start(xw[:], x_words[0].rearrange("p t r -> p (t r)").bitcast(I32))
+        sync.dma_start(xw[:], x_words[0].rearrange("p t r -> p (t r)").bitcast(I32))
         make_identity(nc, ident[:])
         plane = {name: zeroed_plane(name, E) for name in ("w1", "w3", "w2")}
-        load_scales([sync] * 4, "w1", plane["w1"], 0, E)
-        load_scales([scalar] * 3 + [sync], "w3", plane["w3"], 0, E)
+        nc.scalar.activation(warm[:], warm[:], SIGMOID)
+        load_scales([scalar] * 4, "w1", plane["w1"], 0, E)
+        load_scales([sync] * 3 + [scalar], "w3", plane["w3"], 0, E)
+        for name, e0, e1 in LATER:
+            load_words(sync, name, word_tile(name, e0, e1), 0, e0, e1)
+            if (name, e0) == ("w2", 0):
+                load_scales([scalar, scalar, sync, sync], "w2", plane["w2"], 0, E)
 
         gathered_words = {}
         gathered_scales = {}
 
         def gather_words(g):
             s0, n = g * WORD_CUT, WORD_CUT
-            tile = ring_gw.tile([P, n], I32, name="gw", align_bytes=64)
+            tile = keep.tile([P, n], I32, name="gw", tag="gw%d" % WORD_TAGS[g], align_bytes=64)
             nc.vector.tensor_copy(
                 tile[:].bitcast(U32), xw[:].bitcast(U32).indirect(offsets[:, s0 // 16 : (s0 + n) // 16])
             )
@@ -121,8 +111,8 @@ def tile_moe_pke_glu_sigmoid_kernel(
                 gathered_words[s0 // P + u] = tile[:, u * P : (u + 1) * P]
 
         def gather_scales(g):
-            s0, n = g * SCALE_CUT, SCALE_CUT
-            tile = ring_gs.tile([P, n], U8, name="gs", align_bytes=64)
+            s0, n = sum(SCALE_CUTS[:g]), SCALE_CUTS[g]
+            tile = keep.tile([P, n], U8, name="gs", tag="gs%d" % SCALE_TAGS[g], align_bytes=64)
             nc.vector.tensor_copy(tile[:], xs[:].bitcast(U8).indirect(offsets[:, s0 // 16 : (s0 + n) // 16]))
             for u in range(n // P):
                 gathered_scales[s0 // P + u] = tile[:, u * P : (u + 1) * P]
@@ -141,7 +131,7 @@ def tile_moe_pke_glu_sigmoid_kernel(
             u = ORDER[k]
             e = u // 2
             name = {"a": "w1", "b": "w3"}[kind]
-            acc = psum.tile([P, H], F32, name=kind, bufs={"a": 2, "b": 3}[kind])
+            acc = psum.tile([P, H], F32, name=kind, bufs=BANKS[kind])
             nc.tensor.matmul_mx(
                 acc[:],
                 lhsT=gathered_words[u].bitcast(FP8X4),
@@ -176,8 +166,8 @@ def tile_moe_pke_glu_sigmoid_kernel(
             )
             held["h", k] = h
 
-        def turn(ks):
-            turned = psum.tile([P, len(ks), 2, P], F32, name="t", bufs=TB)
+        def turn(ks, tag="t"):
+            turned = psum.tile([P, len(ks), 2, P], F32, name="t", tag=tag, bufs=BANKS[tag])
             for half in reversed(range(len(ks))):
                 pairs = held["h", ks[half]][:].bitcast(F32)
                 for v in range(2):
@@ -199,13 +189,13 @@ def tile_moe_pke_glu_sigmoid_kernel(
         def one_expert(g):
             return ORDER[2 * g] // 2 == ORDER[2 * g + 1] // 2
 
-        def second(ks):
+        def second(ks, tag="y"):
             codes, scales = held["q", ks]
             g = ks[0] // 2
             n = 2 * P if one_expert(g) and len(ks) == 2 else P
             for half in range(2):
                 if ks[0] % 2 == 0:
-                    held["y", g, half] = psum.tile([P, 2, 2 * P], F32, name="y", bufs=YB)
+                    held["y", g, half] = psum.tile([P, 2, 2 * P], F32, name="y", tag=tag, bufs=BANKS[tag])
                 y = held["y", g, half]
                 for j in range(2):
                     t = 2 * half + j
@@ -246,33 +236,49 @@ def tile_moe_pke_glu_sigmoid_kernel(
                     nc.sync.dma_start(rows[:, t, ms, cols], result[:, t, ms, cols])
 
         G = UNITS // 2
-        parts = [(2 * g, 2 * g + 1) for g in range(G - 1)] + LAST
-        calls = []
-        for k in range(UNITS):
-            calls.append((k - LEAD_A, first, ("a", k)))
-            calls.append((k, sigmoid, (k,)))
-            calls.append((k + LAG_G - LEAD_B, first, ("b", k)))
-            calls.append((k + LAG_G, gate, (k,)))
-        for ks in parts:
-            k = ks[-1] + LAG_G
-            g = ks[0] // 2
-            calls.append((k + LAG_T, turn, (ks,)))
-            calls.append((k + LAG_C, collect, (ks, COLLECT[g])))
-            calls.append((k + LAG_Q, quantise, (ks,)))
-            calls.append((k + LAG_Y, second, (ks,)))
-            if ks[-1] % 2 == 1:
-                calls.append((k + LAG_E0, empty, (g, 0, EMPTY0[g])))
-                calls.append((k + LAG_E1, empty, (g, 1, EMPTY1[g])))
-        calls.append((W3, gather_words, (3,)))
+        pair = [(2 * g, 2 * g + 1) for g in range(G)]
         gather_scales(0)
-        later = keep.tile([P, 14 * 1024], U8, name="later_words", tag="xs", align_bytes=64)
-        slot = 0
-        for name, e0, e1 in LATER:
-            load_words(sync, name, later, slot, e0, e1)
-            slot = slot + e1 - e0
-            if (name, e0) == ("w2", 0):
-                load_scales([scalar, scalar, sync, sync], "w2", plane["w2"], 0, E)
+        gather_scales(1)
         for c in range(3):
             gather_words(c)
-        for when, call, args in sorted(calls, key=lambda c: c[0]):
-            call(*args)
+        first("a", 0)
+        first("a", 1)
+        first("b", 0)
+        for g in range(G):
+            sigmoid(2 * g)
+            if g >= 1:
+                turn(pair[g - 1])
+            if g >= 2:
+                second(pair[g - 2])
+            first("b", 2 * g + 1)
+            first("a", 2 * g + 2)
+            if g >= 1:
+                collect(pair[g - 1], "A")
+            gate(2 * g)
+            if g >= 2:
+                empty(g - 2, 0, EMPTY0[g - 2])
+            sigmoid(2 * g + 1)
+            if g >= 1:
+                quantise(pair[g - 1])
+            first("b", 2 * g + 2)
+            if g == 2:
+                gather_scales(2)
+            if g == 3:
+                gather_words(3)
+            first("a", 2 * g + 3)
+            if g >= 2:
+                empty(g - 2, 1, "A")
+            gate(2 * g + 1)
+        last = [(k,) for k in pair[G - 1]]
+        turn(last[0])
+        turn(last[1], "b")
+        collect(last[0], "A")
+        collect(last[1], "A")
+        second(pair[G - 2])
+        quantise(last[0])
+        quantise(last[1])
+        second(last[0], "a")
+        second(last[1], "a")
+        for g in (G - 2, G - 1):
+            empty(g, 0, "V")
+            empty(g, 1, "A")

@@ -21,12 +21,12 @@ MULT = mybir.AluOpType.mult
 P = 128
 UNITS = S // P
 WORD_CUT = 384
-WORD_TAGS = (0, 1, 2, 1)
+WORD_TAGS = (0, 1, 2, 3)
 SCALE_CUTS = (640, 384, 512)
 SCALE_TAGS = (0, 1, 0)
 LATER = (("w1", 2, 4), ("w3", 2, 4), ("w2", 0, 2), ("w1", 4, 6), ("w3", 4, 6), ("w2", 2, 6))
 BANKS = {"a": 2, "b": 3, "t": 1, "y": 2}
-EMPTY0 = "AVVVVV"
+EMPTY0 = "VVVVVV"
 QUADRANTS = (0, 2, 1, 3)
 ORDER = [0, 1, 2, 3, 4, 6, 5, 7, 8, 10, 9, 11]
 
@@ -68,9 +68,9 @@ def tile_moe_pke_glu_sigmoid_kernel(
             for e in range(e0, e1):
                 planes[name, e] = tile[:, (e - e0) * 512 : (e - e0 + 1) * 512]
 
-        def zeroed_plane(name, experts):
-            tile = keep.tile([P, experts * 512], U8, name=name + "_plane", align_bytes=64)
-            nc.vector.memset(tile[:].bitcast(I32), 0)
+        def zeroed_plane(engine, name, tag):
+            tile = keep.tile([P, E * 512], U8, name=name + "_plane", tag=tag, align_bytes=64)
+            engine.memset(tile[:].bitcast(I32), 0)
             return tile
 
         sync, scalar = nc.sync, nc.scalar
@@ -79,8 +79,7 @@ def tile_moe_pke_glu_sigmoid_kernel(
         def word_tile(name, e0, e1):
             return keep.tile([P, (e1 - e0) * 1024], U8, name="%s_words%d" % (name, e0), align_bytes=64)
 
-        load_words(scalar, "w1", word_tile("w1", 0, 2), 0, 0, 2)
-        load_words(sync, "w3", word_tile("w3", 0, 2), 0, 0, 2)
+        load_words(sync, "w1", word_tile("w1", 0, 2), 0, 0, 2)
         nc.vector.memset(xs[:], 0)
         warm = keep.tile([P, 1], F32, name="warm")
         nc.vector.memset(warm[:], 0.0)
@@ -89,15 +88,12 @@ def tile_moe_pke_glu_sigmoid_kernel(
         xw = keep.tile([P, T], I32, name="xw", align_bytes=64)
         sync.dma_start(xw[:], x_words[0].rearrange("p t r -> p (t r)").bitcast(I32))
         make_identity(nc, ident[:])
-        plane = {name: zeroed_plane(name, E) for name in ("w1", "w3", "w2")}
         nc.scalar.activation(warm[:], warm[:], SIGMOID)
-        load_scales([scalar] * 4, "w1", plane["w1"], 0, E)
-        load_scales([sync] * 3 + [scalar], "w3", plane["w3"], 0, E)
-        for name, e0, e1 in LATER:
-            load_words(sync, name, word_tile(name, e0, e1), 0, e0, e1)
-            if (name, e0) == ("w2", 0):
-                load_scales([scalar, scalar, sync, sync], "w2", plane["w2"], 0, E)
+        load_scales([sync] * 4, "w1", zeroed_plane(nc.vector, "w1", "w1_plane"), 0, E)
+        load_words(sync, "w3", word_tile("w3", 0, 2), 0, 0, 2)
+        load_scales([sync] * 4, "w3", zeroed_plane(nc.vector, "w3", "w3_plane"), 0, E)
 
+        held = {}
         gathered_words = {}
         gathered_scales = {}
 
@@ -114,10 +110,9 @@ def tile_moe_pke_glu_sigmoid_kernel(
             s0, n = sum(SCALE_CUTS[:g]), SCALE_CUTS[g]
             tile = keep.tile([P, n], U8, name="gs", tag="gs%d" % SCALE_TAGS[g], align_bytes=64)
             nc.vector.tensor_copy(tile[:], xs[:].bitcast(U8).indirect(offsets[:, s0 // 16 : (s0 + n) // 16]))
+            held["gs", g] = tile
             for u in range(n // P):
                 gathered_scales[s0 // P + u] = tile[:, u * P : (u + 1) * P]
-
-        held = {}
 
         def copy(engine, dst, src):
             if engine == "V":
@@ -125,13 +120,14 @@ def tile_moe_pke_glu_sigmoid_kernel(
             else:
                 nc.scalar.copy(dst, src)
 
-        def first(kind, k):
+        def first(kind, k, tag=None):
             if k >= UNITS:
                 return
             u = ORDER[k]
             e = u // 2
             name = {"a": "w1", "b": "w3"}[kind]
-            acc = psum.tile([P, H], F32, name=kind, bufs=BANKS[kind])
+            tag = tag or kind
+            acc = psum.tile([P, H], F32, name=kind, tag=tag, bufs=BANKS[tag])
             nc.tensor.matmul_mx(
                 acc[:],
                 lhsT=gathered_words[u].bitcast(FP8X4),
@@ -238,47 +234,69 @@ def tile_moe_pke_glu_sigmoid_kernel(
         G = UNITS // 2
         pair = [(2 * g, 2 * g + 1) for g in range(G)]
         gather_scales(0)
+        blank = keep.tile([P, 4 * P], BF16, name="blank", align_bytes=64)
+        blank_codes = keep.tile([P, P], U32, name="blank_codes", align_bytes=64)
+        blank_scales = keep.tile([P, P], U8, name="blank_scales", align_bytes=64)
+        nc.gpsimd.memset(blank[:], 0.0)
+        nc.vector.quantize_mx(blank_codes[:].bitcast(FP8X4), blank_scales[:], blank[:])
+        unread = psum.tile([P, H], F32, name="unread", tag="t", bufs=BANKS["t"])
+        for n in range(3):
+            nc.tensor.matmul_mx(
+                unread[:],
+                lhsT=blank_codes[:].bitcast(FP8X4),
+                lhsT_scale=blank_scales[:],
+                rhs=words["w1", 0].bitcast(FP4X4),
+                rhs_scale=held["gs", 0][:, 0:512],
+                start=True,
+                stop=True,
+            )
+        for name, e0, e1 in LATER:
+            load_words(sync, name, word_tile(name, e0, e1), 0, e0, e1)
+            if (name, e0) == ("w2", 0):
+                load_scales([nc.gpsimd] * 2 + [sync] * 2, "w2", zeroed_plane(nc.gpsimd, "w2", "blank_codes"), 0, E)
         gather_scales(1)
         for c in range(3):
             gather_words(c)
         first("a", 0)
         first("a", 1)
         first("b", 0)
+        first("b", 1)
         for g in range(G):
             sigmoid(2 * g)
+            if g >= 2:
+                quantise(pair[g - 2])
             if g >= 1:
                 turn(pair[g - 1])
-            if g >= 2:
-                second(pair[g - 2])
-            first("b", 2 * g + 1)
-            first("a", 2 * g + 2)
-            if g >= 1:
-                collect(pair[g - 1], "A")
+            sigmoid(2 * g + 1)
             gate(2 * g)
             if g >= 2:
-                empty(g - 2, 0, EMPTY0[g - 2])
-            sigmoid(2 * g + 1)
+                second(pair[g - 2])
             if g >= 1:
-                quantise(pair[g - 1])
-            first("b", 2 * g + 2)
+                collect(pair[g - 1], "A")
+            if g >= 2:
+                empty(g - 2, 0, EMPTY0[g - 2])
+            first("a", 2 * g + 2)
+            if g >= 2:
+                empty(g - 2, 1, "A")
             if g == 2:
                 gather_scales(2)
             if g == 3:
                 gather_words(3)
             first("a", 2 * g + 3)
-            if g >= 2:
-                empty(g - 2, 1, "A")
             gate(2 * g + 1)
+            first("b", 2 * g + 2)
+            first("b", 2 * g + 3)
         last = [(k,) for k in pair[G - 1]]
+        quantise(pair[G - 2])
         turn(last[0])
         turn(last[1], "b")
         collect(last[0], "A")
         collect(last[1], "A")
-        second(pair[G - 2])
+        second(pair[G - 2], "a")
         quantise(last[0])
         quantise(last[1])
-        second(last[0], "a")
-        second(last[1], "a")
+        second(last[0], "b")
+        second(last[1], "b")
         for g in (G - 2, G - 1):
             empty(g, 0, "V")
             empty(g, 1, "A")

@@ -27,7 +27,6 @@ SCALE_TAGS = (0, 1, 0)
 LATER = (("w1", 2, 4), ("w3", 2, 4), ("w2", 0, 2), ("w1", 4, 6), ("w3", 4, 6), ("w2", 2, 6))
 BANKS = {"a": 2, "b": 3, "t": 1, "y": 2}
 EMPTY0 = "VVVVVV"
-QUADRANTS = (0, 2, 1, 3)
 ORDER = [0, 1, 2, 3, 4, 6, 5, 7, 8, 10, 9, 11]
 
 def tile_moe_pke_glu_sigmoid_kernel(
@@ -60,10 +59,10 @@ def tile_moe_pke_glu_sigmoid_kernel(
                 words[name, e] = part[:, (e - e0) * 1024 : (e - e0 + 1) * 1024]
 
         def load_scales(queues, name, tile, e0, e1):
-            for j, q in enumerate(QUADRANTS):
+            for j in range(4):
                 queues[j].dma_start(
-                    tile[32 * q : 32 * q + 4, : (e1 - e0) * 512].bitcast(I32).rearrange("p (e w) -> p e w", e=e1 - e0),
-                    dram_scales[name][e0:e1, 0, 4 * q : 4 * q + 4, :].rearrange("e q b -> q e b").bitcast(I32),
+                    tile[j:P:32, : (e1 - e0) * 512].bitcast(I32).rearrange("p (e w) -> p e w", e=e1 - e0),
+                    dram_scales[name][e0:e1, 0, j:16:4, :].rearrange("e q b -> q e b").bitcast(I32),
                 )
             for e in range(e0, e1):
                 planes[name, e] = tile[:, (e - e0) * 512 : (e - e0 + 1) * 512]
@@ -81,14 +80,11 @@ def tile_moe_pke_glu_sigmoid_kernel(
 
         load_words(sync, "w1", word_tile("w1", 0, 2), 0, 0, 2)
         nc.vector.memset(xs[:], 0)
-        warm = keep.tile([P, 1], F32, name="warm")
-        nc.vector.memset(warm[:], 0.0)
-        for queue, q in zip((scalar, sync, scalar, sync), QUADRANTS):
-            queue.dma_start(xs[32 * q : 32 * q + 4, :], x_scales[0, 4 * q : 4 * q + 4, :].bitcast(I32))
+        for j, queue in enumerate((scalar, sync, scalar, sync)):
+            queue.dma_start(xs[j:P:32, :], x_scales[0, j:16:4, :].bitcast(I32))
         xw = keep.tile([P, T], I32, name="xw", align_bytes=64)
         sync.dma_start(xw[:], x_words[0].rearrange("p t r -> p (t r)").bitcast(I32))
         make_identity(nc, ident[:])
-        nc.scalar.activation(warm[:], warm[:], SIGMOID)
         load_scales([sync] * 4, "w1", zeroed_plane(nc.vector, "w1", "w1_plane"), 0, E)
         load_words(sync, "w3", word_tile("w3", 0, 2), 0, 0, 2)
         load_scales([sync] * 4, "w3", zeroed_plane(nc.vector, "w3", "w3_plane"), 0, E)

@@ -27,7 +27,7 @@ SCALE_TAGS = (0, 1, 0)
 LATER = (("w1", 2, 4), ("w3", 2, 4), ("w2", 0, 2), ("w1", 4, 6), ("w3", 4, 6), ("w2", 2, 6))
 BANKS = {"a": 2, "b": 3, "t": 1, "y": 2}
 EMPTY0 = "VVVVVV"
-ORDER = [0, 1, 2, 3, 4, 6, 5, 7, 8, 10, 9, 11]
+ORDER = [0, 2, 1, 3, 4, 6, 5, 7, 8, 10, 9, 11]
 
 def tile_moe_pke_glu_sigmoid_kernel(
     tc, x_words, x_scales, w1_words, w1_scales, w3_words, w3_scales, w2_words, w2_scales, offs, out

@@ -20,14 +20,19 @@ MULT = mybir.AluOpType.mult
 
 P = 128
 UNITS = S // P
+PAIRS = UNITS // 2
 WORD_CUT = 384
-WORD_TAGS = (0, 1, 2, 3)
-SCALE_CUTS = (640, 384, 512)
-SCALE_TAGS = (0, 1, 0)
-LATER = (("w1", 2, 4), ("w3", 2, 4), ("w2", 0, 2), ("w1", 4, 6), ("w3", 4, 6), ("w2", 2, 6))
-BANKS = {"a": 2, "b": 3, "t": 1, "y": 2}
-EMPTY0 = "VVVVVV"
-ORDER = [0, 2, 1, 3, 4, 6, 5, 7, 8, 10, 9, 11]
+SCALE_CUTS = (640, 512, 384)
+LATER = (("w1", 2, 4), ("w3", 2, 4), ("w2", 0, 2), ("w1", 4, 6), ("w2", 2, 4), ("w3", 4, 6), ("w2", 4, 6))
+VECTOR_TILES = 36
+SCALAR_TILES = 30
+WARM = 3
+
+
+def unit_at(k):
+    e, half = 2 * (k // 4) + k % 2, k // 2 % 2
+    return 2 * e + half
+
 
 def tile_moe_pke_glu_sigmoid_kernel(
     tc, x_words, x_scales, w1_words, w1_scales, w3_words, w3_scales, w2_words, w2_scales, offs, out
@@ -35,11 +40,17 @@ def tile_moe_pke_glu_sigmoid_kernel(
     nc = tc.nc
     with ExitStack() as ctx:
         keep = ctx.enter_context(tc.tile_pool(name="keep", bufs=1))
-        ring_sig = ctx.enter_context(tc.tile_pool(name="ring_sig", bufs=4))
-        ring_h = ctx.enter_context(tc.tile_pool(name="ring_h", bufs=4))
-        ring_ht = ctx.enter_context(tc.tile_pool(name="ring_ht", bufs=2))
-        ring_q = ctx.enter_context(tc.tile_pool(name="ring_q", bufs=2))
-        psum = ctx.enter_context(tc.psum_pool(name="psum", bufs=2))
+        line = ctx.enter_context(tc.tile_pool(name="line", bufs=1))
+        psum = ctx.enter_context(tc.psum_pool(name="psum", bufs=8))
+
+        def by_vector(shape, dtype, name):
+            return line.tile(shape, dtype, name=name, tag="vector", bufs=VECTOR_TILES, align_bytes=64)
+
+        def by_scalar(shape, dtype, name):
+            return line.tile(shape, dtype, name=name, tag="scalar", bufs=SCALAR_TILES, align_bytes=64)
+
+        def bank(shape, name):
+            return psum.tile(shape, F32, name=name, tag="bank")
 
         offsets = keep.tile([P, S // 16], U16, name="offsets")
         xs = keep.tile([P, T // 4], I32, name="xs", align_bytes=64)
@@ -49,23 +60,23 @@ def tile_moe_pke_glu_sigmoid_kernel(
         words = {}
         planes = {}
 
-        def load_words(queue, name, tile, slot, e0, e1):
-            part = tile[:, slot * 1024 : (slot + e1 - e0) * 1024]
-            queue.dma_start(
-                part.bitcast(I32).rearrange("p (e w) -> p e w", e=e1 - e0),
+        def load_words(name, e0, e1):
+            tile = keep.tile([P, (e1 - e0) * 1024], U8, name="%s_words%d" % (name, e0), align_bytes=64)
+            nc.sync.dma_start(
+                tile[:].bitcast(I32).rearrange("p (e w) -> p e w", e=e1 - e0),
                 dram_words[name][e0:e1, 0].rearrange("e p b -> p e b").bitcast(I32),
             )
             for e in range(e0, e1):
-                words[name, e] = part[:, (e - e0) * 1024 : (e - e0 + 1) * 1024]
+                words[name, e] = tile[:, (e - e0) * 1024 : (e - e0 + 1) * 1024]
 
-        def load_scales(queues, name, tile, e0, e1):
+        def load_scales(queues, name, tile):
             for j in range(4):
                 queues[j].dma_start(
-                    tile[j:P:32, : (e1 - e0) * 512].bitcast(I32).rearrange("p (e w) -> p e w", e=e1 - e0),
-                    dram_scales[name][e0:e1, 0, j:16:4, :].rearrange("e q b -> q e b").bitcast(I32),
+                    tile[j:P:32, :].bitcast(I32).rearrange("p (e w) -> p e w", e=E),
+                    dram_scales[name][:, 0, j:16:4, :].rearrange("e q b -> q e b").bitcast(I32),
                 )
-            for e in range(e0, e1):
-                planes[name, e] = tile[:, (e - e0) * 512 : (e - e0 + 1) * 512]
+            for e in range(E):
+                planes[name, e] = tile[:, e * 512 : (e + 1) * 512]
 
         def zeroed_plane(engine, name, tag):
             tile = keep.tile([P, E * 512], U8, name=name + "_plane", tag=tag, align_bytes=64)
@@ -74,20 +85,17 @@ def tile_moe_pke_glu_sigmoid_kernel(
 
         sync, scalar = nc.sync, nc.scalar
         nc.sync.dma_start(offsets[:], offs)
-
-        def word_tile(name, e0, e1):
-            return keep.tile([P, (e1 - e0) * 1024], U8, name="%s_words%d" % (name, e0), align_bytes=64)
-
-        load_words(sync, "w1", word_tile("w1", 0, 2), 0, 0, 2)
+        load_words("w1", 0, 1)
         nc.vector.memset(xs[:], 0)
         for j, queue in enumerate((scalar, sync, scalar, sync)):
             queue.dma_start(xs[j:P:32, :], x_scales[0, j:16:4, :].bitcast(I32))
         xw = keep.tile([P, T], I32, name="xw", align_bytes=64)
         sync.dma_start(xw[:], x_words[0].rearrange("p t r -> p (t r)").bitcast(I32))
         make_identity(nc, ident[:])
-        load_scales([sync] * 4, "w1", zeroed_plane(nc.vector, "w1", "w1_plane"), 0, E)
-        load_words(sync, "w3", word_tile("w3", 0, 2), 0, 0, 2)
-        load_scales([sync] * 4, "w3", zeroed_plane(nc.vector, "w3", "w3_plane"), 0, E)
+        load_scales([sync] * 4, "w1", zeroed_plane(nc.vector, "w1", "w1_plane"))
+        load_words("w1", 1, 2)
+        load_words("w3", 0, 2)
+        load_scales([sync] * 4, "w3", zeroed_plane(nc.vector, "w3", "w3_plane"))
 
         held = {}
         gathered_words = {}
@@ -95,7 +103,7 @@ def tile_moe_pke_glu_sigmoid_kernel(
 
         def gather_words(g):
             s0, n = g * WORD_CUT, WORD_CUT
-            tile = keep.tile([P, n], I32, name="gw", tag="gw%d" % WORD_TAGS[g], align_bytes=64)
+            tile = by_vector([P, n], I32, "gw")
             nc.vector.tensor_copy(
                 tile[:].bitcast(U32), xw[:].bitcast(U32).indirect(offsets[:, s0 // 16 : (s0 + n) // 16])
             )
@@ -104,32 +112,24 @@ def tile_moe_pke_glu_sigmoid_kernel(
 
         def gather_scales(g):
             s0, n = sum(SCALE_CUTS[:g]), SCALE_CUTS[g]
-            tile = keep.tile([P, n], U8, name="gs", tag="gs%d" % SCALE_TAGS[g], align_bytes=64)
+            tile = by_vector([P, n], U8, "gs")
             nc.vector.tensor_copy(tile[:], xs[:].bitcast(U8).indirect(offsets[:, s0 // 16 : (s0 + n) // 16]))
             held["gs", g] = tile
             for u in range(n // P):
                 gathered_scales[s0 // P + u] = tile[:, u * P : (u + 1) * P]
 
-        def copy(engine, dst, src):
-            if engine == "V":
-                nc.vector.tensor_copy(dst, src)
-            else:
-                nc.scalar.copy(dst, src)
-
-        def first(kind, k, tag=None):
+        def first(kind, k):
             if k >= UNITS:
                 return
-            u = ORDER[k]
-            e = u // 2
+            u = unit_at(k)
             name = {"a": "w1", "b": "w3"}[kind]
-            tag = tag or kind
-            acc = psum.tile([P, H], F32, name=kind, tag=tag, bufs=BANKS[tag])
+            acc = bank([P, H], kind)
             nc.tensor.matmul_mx(
                 acc[:],
                 lhsT=gathered_words[u].bitcast(FP8X4),
                 lhsT_scale=gathered_scales[u],
-                rhs=words[name, e].bitcast(FP4X4),
-                rhs_scale=planes[name, e],
+                rhs=words[name, u // 2].bitcast(FP4X4),
+                rhs_scale=planes[name, u // 2],
                 start=True,
                 stop=True,
             )
@@ -138,7 +138,7 @@ def tile_moe_pke_glu_sigmoid_kernel(
         def sigmoid(k):
             if k >= UNITS:
                 return
-            sig = ring_sig.tile([P, H], F32, name="sig", align_bytes=64)
+            sig = by_scalar([P, H], F32, "sig")
             nc.scalar.activation(
                 sig[:].rearrange("s (v p d) -> s v p d", v=2, d=2),
                 held["a", k][:].rearrange("s (p v d) -> s v p d", v=2, d=2),
@@ -147,9 +147,9 @@ def tile_moe_pke_glu_sigmoid_kernel(
             held["sig", k] = sig
 
         def gate(k):
-            if not 0 <= k < UNITS:
+            if k >= UNITS:
                 return
-            h = ring_h.tile([P, H], BF16, name="h", align_bytes=64)
+            h = by_vector([P, H], BF16, "h")
             nc.vector.tensor_tensor(
                 h[:].rearrange("s (v p d) -> s v p d", v=2, d=2),
                 held["b", k][:].rearrange("s (p v d) -> s v p d", v=2, d=2),
@@ -158,85 +158,71 @@ def tile_moe_pke_glu_sigmoid_kernel(
             )
             held["h", k] = h
 
-        def turn(ks, tag="t"):
-            turned = psum.tile([P, len(ks), 2, P], F32, name="t", tag=tag, bufs=BANKS[tag])
+        def turn(ks):
+            turned = bank([P, len(ks), 2, P], "t")
             for half in reversed(range(len(ks))):
                 pairs = held["h", ks[half]][:].bitcast(F32)
                 for v in range(2):
                     nc.tensor.transpose(turned[:, half, v, :], pairs[:, v * P : (v + 1) * P], ident[:])
             held["t", ks] = turned
 
-        def collect(ks, engine):
-            ht = ring_ht.tile([P, 4 * P * len(ks)], BF16, name="ht", align_bytes=64)
+        def collect(ks):
+            ht = by_scalar([P, 4 * P * len(ks)], BF16, "ht")
             dst = ht[:].bitcast(F32).rearrange("p (a s v) -> p a s v", a=len(ks), v=2)
-            copy(engine, dst, held["t", ks][:].rearrange("p a v s -> p a s v"))
+            nc.scalar.copy(dst, held["t", ks][:].rearrange("p a v s -> p a s v"))
             held["ht", ks] = ht
 
         def quantise(ks):
-            codes = ring_q.tile([P, P * len(ks)], U32, name="codes", align_bytes=64)
-            scales = ring_q.tile([P, P * len(ks)], U8, name="scales", align_bytes=64)
+            codes = by_vector([P, P * len(ks)], U32, "codes")
+            scales = keep.tile([P, P * len(ks)], U8, name="scales%d" % ks[0], align_bytes=64)
             nc.vector.quantize_mx(codes[:].bitcast(FP8X4), scales[:], held["ht", ks][:])
-            held["q", ks] = (codes, scales)
+            for c, k in enumerate(ks):
+                held["q", k] = (codes[:, c * P : (c + 1) * P], scales[:, c * P : (c + 1) * P])
 
-        def one_expert(g):
-            return ORDER[2 * g] // 2 == ORDER[2 * g + 1] // 2
+        def second(g, half, ks):
+            if ks[0] % 2 == 0:
+                held["y", g, half] = bank([P, 2, 2 * P], "y")
+            y = held["y", g, half]
+            for j in range(2):
+                t = 2 * half + j
+                for k in ks:
+                    codes, scales = held["q", k]
+                    e = unit_at(k) // 2
+                    nc.tensor.matmul_mx(
+                        y[:, j, k % 2 * P : (k % 2 + 1) * P],
+                        lhsT=words["w2", e][:, t * 256 : (t + 1) * 256].bitcast(FP4X4),
+                        lhsT_scale=planes["w2", e][:, t * P : (t + 1) * P],
+                        rhs=codes.bitcast(FP8X4),
+                        rhs_scale=scales,
+                        start=True,
+                        stop=True,
+                    )
 
-        def second(ks, tag="y"):
-            codes, scales = held["q", ks]
-            g = ks[0] // 2
-            n = 2 * P if one_expert(g) and len(ks) == 2 else P
-            for half in range(2):
-                if ks[0] % 2 == 0:
-                    held["y", g, half] = psum.tile([P, 2, 2 * P], F32, name="y", tag=tag, bufs=BANKS[tag])
-                y = held["y", g, half]
-                for j in range(2):
-                    t = 2 * half + j
-                    for c0 in range(0, P * len(ks), n):
-                        k = ks[c0 // P]
-                        e = ORDER[k] // 2
-                        nc.tensor.matmul_mx(
-                            y[:, j, k % 2 * P : k % 2 * P + n],
-                            lhsT=words["w2", e][:, t * 256 : (t + 1) * 256].bitcast(FP4X4),
-                            lhsT_scale=planes["w2", e][:, t * P : (t + 1) * P],
-                            rhs=codes[:, c0 : c0 + n].bitcast(FP8X4),
-                            rhs_scale=scales[:, c0 : c0 + n],
-                            start=True,
-                            stop=True,
-                        )
-
-        result = keep.tile([P, 4, R, E * 64], F32, name="result", align_bytes=64)
         rows = out.rearrange("(t p) (m c) -> p t m c", p=P, m=R)
 
         def empty(g, half, engine):
-            ts = (2 * half, 2 * half + 1)
-            u = ORDER[2 * g]
-            e = u // 2
-            if one_expert(g):
-                src = held["y", g, half][:].rearrange("p k (m c) -> p k m c", c=64)
-                copy(engine, result[:, ts[0] : ts[1] + 1, :, 64 * e : 64 * e + 64], src)
-                if e % 2 == 1:
-                    cols = slice(64 * (e - 1), 64 * (e + 1))
-                    for t in ts:
-                        nc.sync.dma_start(rows[:, t, :, cols], result[:, t, :, cols])
+            u = unit_at(2 * g)
+            ranks = slice(2 * (u % 2), 2 * (u % 2) + 2)
+            cols = slice(64 * (u // 2), 64 * (u // 2 + 2))
+            src = held["y", g, half][:].rearrange("p j (e m c) -> p j m e c", e=2, c=64)
+            if engine == "V":
+                result = by_vector([P, 2, 2, P], F32, "result")
+                nc.vector.tensor_copy(result[:].rearrange("p j m (e c) -> p j m e c", e=2), src)
             else:
-                ms = slice(2 * (u % 2), 2 * (u % 2) + 2)
-                cols = slice(64 * e, 64 * (e + 2))
-                src = held["y", g, half][:].rearrange("p k (e m c) -> p k m e c", e=2, c=64)
-                dst = result[:, ts[0] : ts[1] + 1, ms, cols].rearrange("p k m (e c) -> p k m e c", e=2)
-                copy(engine, dst, src)
-                for t in ts:
-                    nc.sync.dma_start(rows[:, t, ms, cols], result[:, t, ms, cols])
+                result = by_scalar([P, 2, 2, P], F32, "result")
+                nc.scalar.copy(result[:].rearrange("p j m (e c) -> p j m e c", e=2), src)
+            for j in range(2):
+                nc.sync.dma_start(rows[:, 2 * half + j, ranks, cols], result[:, j])
 
-        G = UNITS // 2
-        pair = [(2 * g, 2 * g + 1) for g in range(G)]
-        gather_scales(0)
+        pair = [(2 * g, 2 * g + 1) for g in range(PAIRS)]
         blank = keep.tile([P, 4 * P], BF16, name="blank", align_bytes=64)
         blank_codes = keep.tile([P, P], U32, name="blank_codes", align_bytes=64)
         blank_scales = keep.tile([P, P], U8, name="blank_scales", align_bytes=64)
         nc.gpsimd.memset(blank[:], 0.0)
         nc.vector.quantize_mx(blank_codes[:].bitcast(FP8X4), blank_scales[:], blank[:])
-        unread = psum.tile([P, H], F32, name="unread", tag="t", bufs=BANKS["t"])
-        for n in range(3):
+        gather_scales(0)
+        unread = bank([P, H], "unread")
+        for n in range(WARM):
             nc.tensor.matmul_mx(
                 unread[:],
                 lhsT=blank_codes[:].bitcast(FP8X4),
@@ -247,52 +233,51 @@ def tile_moe_pke_glu_sigmoid_kernel(
                 stop=True,
             )
         for name, e0, e1 in LATER:
-            load_words(sync, name, word_tile(name, e0, e1), 0, e0, e1)
+            load_words(name, e0, e1)
             if (name, e0) == ("w2", 0):
-                load_scales([nc.gpsimd] * 2 + [sync] * 2, "w2", zeroed_plane(nc.gpsimd, "w2", "blank_codes"), 0, E)
+                load_scales([nc.gpsimd] * 2 + [sync] * 2, "w2", zeroed_plane(nc.gpsimd, "w2", "blank_codes"))
         gather_scales(1)
-        for c in range(3):
-            gather_words(c)
-        first("a", 0)
-        first("a", 1)
-        first("b", 0)
-        first("b", 1)
-        for g in range(G):
-            sigmoid(2 * g)
-            if g >= 2:
-                quantise(pair[g - 2])
+        gather_words(0)
+        gather_words(1)
+        for k in range(4):
+            first("a", k)
+            sigmoid(k)
+        gather_words(2)
+        gather_words(3)
+        for k in range(2):
+            first("b", k)
+        for g in range(-1, PAIRS - 1):
+            gate(2 * g + 2)
+            gate(2 * g + 3)
+            if g >= 0:
+                turn(pair[g])
+                collect(pair[g])
             if g >= 1:
-                turn(pair[g - 1])
-            sigmoid(2 * g + 1)
-            gate(2 * g)
-            if g >= 2:
-                second(pair[g - 2])
-            if g >= 1:
-                collect(pair[g - 1], "A")
-            if g >= 2:
-                empty(g - 2, 0, EMPTY0[g - 2])
-            first("a", 2 * g + 2)
-            if g >= 2:
-                empty(g - 2, 1, "A")
-            if g == 2:
+                second(g - 1, 0, pair[g - 1])
+                second(g - 1, 1, pair[g - 1])
+            first("b", 2 * g + 4)
+            first("a", 2 * g + 6)
+            first("b", 2 * g + 5)
+            first("a", 2 * g + 7)
+            if g == -1:
                 gather_scales(2)
-            if g == 3:
-                gather_words(3)
-            first("a", 2 * g + 3)
-            gate(2 * g + 1)
-            first("b", 2 * g + 2)
-            first("b", 2 * g + 3)
-        last = [(k,) for k in pair[G - 1]]
-        quantise(pair[G - 2])
-        turn(last[0])
-        turn(last[1], "b")
-        collect(last[0], "A")
-        collect(last[1], "A")
-        second(pair[G - 2], "a")
-        quantise(last[0])
-        quantise(last[1])
-        second(last[0], "b")
-        second(last[1], "b")
-        for g in (G - 2, G - 1):
-            empty(g, 0, "V")
-            empty(g, 1, "A")
+            if g >= 1:
+                empty(g - 1, 0, "V")
+            if g >= 0:
+                quantise(pair[g])
+            if g >= 1:
+                empty(g - 1, 1, "A")
+            sigmoid(2 * g + 6)
+            sigmoid(2 * g + 7)
+        g = PAIRS - 1
+        turn(pair[g])
+        collect(pair[g])
+        second(g - 1, 0, pair[g - 1])
+        second(g - 1, 1, pair[g - 1])
+        empty(g - 1, 0, "V")
+        quantise(pair[g])
+        empty(g - 1, 1, "A")
+        second(g, 0, pair[g])
+        second(g, 1, pair[g])
+        empty(g, 0, "V")
+        empty(g, 1, "A")

@@ -23,7 +23,7 @@ UNITS = S // P
 PAIRS = UNITS // 2
 WORD_CUT = 384
 SCALE_CUTS = (640, 512, 384)
-LATER = (("w1", 2, 4), ("w3", 2, 4), ("w2", 0, 2), ("w1", 4, 6), ("w2", 2, 4), ("w3", 4, 6), ("w2", 4, 6))
+LATER = (("w1", 2, 4), ("w3", 2, 4), ("w1", 4, 6), ("w2", 0, 2), ("w3", 4, 6), ("w2", 2, 6))
 VECTOR_TILES = 36
 SCALAR_TILES = 30
 WARM = 3
@@ -69,17 +69,17 @@ def tile_moe_pke_glu_sigmoid_kernel(
             for e in range(e0, e1):
                 words[name, e] = tile[:, (e - e0) * 1024 : (e - e0 + 1) * 1024]
 
-        def load_scales(queues, name, tile):
+        def load_scales(queues, name, tile, e0, e1):
             for j in range(4):
                 queues[j].dma_start(
-                    tile[j:P:32, :].bitcast(I32).rearrange("p (e w) -> p e w", e=E),
-                    dram_scales[name][:, 0, j:16:4, :].rearrange("e q b -> q e b").bitcast(I32),
+                    tile[j:P:32, :].bitcast(I32).rearrange("p (e w) -> p e w", e=e1 - e0),
+                    dram_scales[name][e0:e1, 0, j:16:4, :].rearrange("e q b -> q e b").bitcast(I32),
                 )
-            for e in range(E):
-                planes[name, e] = tile[:, e * 512 : (e + 1) * 512]
+            for e in range(e0, e1):
+                planes[name, e] = tile[:, (e - e0) * 512 : (e - e0 + 1) * 512]
 
-        def zeroed_plane(engine, name, tag):
-            tile = keep.tile([P, E * 512], U8, name=name + "_plane", tag=tag, align_bytes=64)
+        def zeroed_plane(engine, name, tag, experts):
+            tile = keep.tile([P, experts * 512], U8, name=name + "_plane", tag=tag, align_bytes=64)
             engine.memset(tile[:].bitcast(I32), 0)
             return tile
 
@@ -92,10 +92,12 @@ def tile_moe_pke_glu_sigmoid_kernel(
         xw = keep.tile([P, T], I32, name="xw", align_bytes=64)
         sync.dma_start(xw[:], x_words[0].rearrange("p t r -> p (t r)").bitcast(I32))
         make_identity(nc, ident[:])
-        load_scales([sync] * 4, "w1", zeroed_plane(nc.vector, "w1", "w1_plane"))
+        load_scales([sync] * 4, "w1", zeroed_plane(nc.vector, "w1", "w1_plane", E), 0, E)
         load_words("w1", 1, 2)
         load_words("w3", 0, 2)
-        load_scales([sync] * 4, "w3", zeroed_plane(nc.vector, "w3", "w3_plane"))
+        load_scales([sync] * 4, "w3", zeroed_plane(nc.vector, "w3", "w3_plane", 2), 0, 2)
+        late_plane = zeroed_plane(nc.vector, "w3", "w3_late_plane", E - 2)
+        w2_plane = zeroed_plane(nc.vector, "w2", "w2_plane", E)
 
         held = {}
         gathered_words = {}
@@ -235,49 +237,68 @@ def tile_moe_pke_glu_sigmoid_kernel(
         for name, e0, e1 in LATER:
             load_words(name, e0, e1)
             if (name, e0) == ("w2", 0):
-                load_scales([nc.gpsimd] * 2 + [sync] * 2, "w2", zeroed_plane(nc.gpsimd, "w2", "blank_codes"))
+                load_scales([sync] * 4, "w2", w2_plane, 0, E)
+            if (name, e0) == ("w3", 2):
+                load_scales([sync] * 4, "w3", late_plane, 2, E)
         gather_scales(1)
+        def sigmoids(ks):
+            for k in ks:
+                first("a", k)
+            for k in ks:
+                sigmoid(k)
+
+        def both_halves(g, ks):
+            second(g, 0, ks)
+            second(g, 1, ks)
+
         gather_words(0)
         gather_words(1)
-        for k in range(4):
-            first("a", k)
-            sigmoid(k)
+        sigmoids(range(0, 4))
         gather_words(2)
-        gather_words(3)
-        for k in range(2):
+        gather_scales(2)
+        for k in range(4):
             first("b", k)
-        for g in range(-1, PAIRS - 1):
-            gate(2 * g + 2)
-            gate(2 * g + 3)
-            if g >= 0:
-                turn(pair[g])
-                collect(pair[g])
-            if g >= 1:
-                second(g - 1, 0, pair[g - 1])
-                second(g - 1, 1, pair[g - 1])
-            first("b", 2 * g + 4)
-            first("a", 2 * g + 6)
-            first("b", 2 * g + 5)
-            first("a", 2 * g + 7)
-            if g == -1:
-                gather_scales(2)
-            if g >= 1:
-                empty(g - 1, 0, "V")
-            if g >= 0:
-                quantise(pair[g])
-            if g >= 1:
-                empty(g - 1, 1, "A")
-            sigmoid(2 * g + 6)
-            sigmoid(2 * g + 7)
+        sigmoids(range(4, 8))
+        for k in range(4):
+            gate(k)
+        gather_words(3)
+        for k in pair[2]:
+            first("b", k)
+        for g in range(2):
+            turn(pair[g])
+            collect(pair[g])
+        for k in pair[2]:
+            gate(k)
+        ready = [0, 1]
+        for g in range(2, PAIRS - 1):
+            for done in ready:
+                quantise(pair[done])
+            for k in pair[g + 1]:
+                first("b", k)
+            sigmoids(range(2 * g + 4, 2 * g + 6))
+            turn(pair[g])
+            collect(pair[g])
+            for done in ready:
+                both_halves(done, pair[done])
+            for k in pair[g + 1]:
+                gate(k)
+            if g < PAIRS - 2:
+                for done in ready:
+                    empty(done, 0, "V")
+                    empty(done, 1, "A")
+            ready = [g]
         g = PAIRS - 1
-        turn(pair[g])
-        collect(pair[g])
-        second(g - 1, 0, pair[g - 1])
-        second(g - 1, 1, pair[g - 1])
-        empty(g - 1, 0, "V")
-        quantise(pair[g])
-        empty(g - 1, 1, "A")
-        second(g, 0, pair[g])
-        second(g, 1, pair[g])
-        empty(g, 0, "V")
-        empty(g, 1, "A")
+        last = [(k,) for k in pair[g]]
+        quantise(pair[g - 1])
+        empty(g - 2, 0, "A")
+        empty(g - 2, 1, "V")
+        for ks in last:
+            turn(ks)
+            collect(ks)
+        both_halves(g - 1, pair[g - 1])
+        for ks in last:
+            quantise(ks)
+            both_halves(g, ks)
+        for done in (g - 1, g):
+            empty(done, 0, "A")
+            empty(done, 1, "V")

@@ -20,18 +20,9 @@ MULT = mybir.AluOpType.mult
 
 P = 128
 UNITS = S // P
-PAIRS = UNITS // 2
-WORD_CUT = 384
-SCALE_CUTS = (640, 512, 384)
-LATER = (("w1", 2, 4), ("w3", 2, 4), ("w1", 4, 6), ("w2", 0, 2), ("w3", 4, 6), ("w2", 2, 6))
-VECTOR_TILES = 36
+VECTOR_TILES = 40
 SCALAR_TILES = 30
-WARM = 3
-
-
-def unit_at(k):
-    e, half = 2 * (k // 4) + k % 2, k // 2 % 2
-    return 2 * e + half
+ORDER = (0, 2, 1, 3, 4, 6, 5, 7, 8, 10, 9, 11)
 
 
 def tile_moe_pke_glu_sigmoid_kernel(
@@ -52,13 +43,14 @@ def tile_moe_pke_glu_sigmoid_kernel(
         def bank(shape, name):
             return psum.tile(shape, F32, name=name, tag="bank")
 
-        offsets = keep.tile([P, S // 16], U16, name="offsets")
-        xs = keep.tile([P, T // 4], I32, name="xs", align_bytes=64)
-        ident = keep.tile([P, P], F32, name="ident", align_bytes=64)
         dram_words = {"w1": w1_words, "w3": w3_words, "w2": w2_words}
         dram_scales = {"w1": w1_scales, "w3": w3_scales, "w2": w2_scales}
         words = {}
         planes = {}
+        cleared = {}
+        held = {}
+        gathered_words = {}
+        gathered_scales = {}
 
         def load_words(name, e0, e1):
             tile = keep.tile([P, (e1 - e0) * 1024], U8, name="%s_words%d" % (name, e0), align_bytes=64)
@@ -69,42 +61,22 @@ def tile_moe_pke_glu_sigmoid_kernel(
             for e in range(e0, e1):
                 words[name, e] = tile[:, (e - e0) * 1024 : (e - e0 + 1) * 1024]
 
-        def load_scales(queues, name, tile, e0, e1):
+        def clear_plane(name, e0, e1):
+            tile = keep.tile([P, (e1 - e0) * 512], U8, name="%s_plane%d" % (name, e0), align_bytes=64)
+            nc.vector.memset(tile[:].bitcast(I32), 0)
+            cleared[name, e0] = tile
+
+        def load_scales(name, e0, e1, queue):
+            tile = cleared[name, e0]
             for j in range(4):
-                queues[j].dma_start(
+                queue.dma_start(
                     tile[j:P:32, :].bitcast(I32).rearrange("p (e w) -> p e w", e=e1 - e0),
                     dram_scales[name][e0:e1, 0, j:16:4, :].rearrange("e q b -> q e b").bitcast(I32),
                 )
             for e in range(e0, e1):
                 planes[name, e] = tile[:, (e - e0) * 512 : (e - e0 + 1) * 512]
 
-        def zeroed_plane(engine, name, tag, experts):
-            tile = keep.tile([P, experts * 512], U8, name=name + "_plane", tag=tag, align_bytes=64)
-            engine.memset(tile[:].bitcast(I32), 0)
-            return tile
-
-        sync, scalar = nc.sync, nc.scalar
-        nc.sync.dma_start(offsets[:], offs)
-        load_words("w1", 0, 1)
-        nc.vector.memset(xs[:], 0)
-        for j, queue in enumerate((scalar, sync, scalar, sync)):
-            queue.dma_start(xs[j:P:32, :], x_scales[0, j:16:4, :].bitcast(I32))
-        xw = keep.tile([P, T], I32, name="xw", align_bytes=64)
-        sync.dma_start(xw[:], x_words[0].rearrange("p t r -> p (t r)").bitcast(I32))
-        make_identity(nc, ident[:])
-        load_scales([sync] * 4, "w1", zeroed_plane(nc.vector, "w1", "w1_plane", E), 0, E)
-        load_words("w1", 1, 2)
-        load_words("w3", 0, 2)
-        load_scales([sync] * 4, "w3", zeroed_plane(nc.vector, "w3", "w3_plane", 2), 0, 2)
-        late_plane = zeroed_plane(nc.vector, "w3", "w3_late_plane", E - 2)
-        w2_plane = zeroed_plane(nc.vector, "w2", "w2_plane", E)
-
-        held = {}
-        gathered_words = {}
-        gathered_scales = {}
-
-        def gather_words(g):
-            s0, n = g * WORD_CUT, WORD_CUT
+        def gather_words(s0, n):
             tile = by_vector([P, n], I32, "gw")
             nc.vector.tensor_copy(
                 tile[:].bitcast(U32), xw[:].bitcast(U32).indirect(offsets[:, s0 // 16 : (s0 + n) // 16])
@@ -112,18 +84,14 @@ def tile_moe_pke_glu_sigmoid_kernel(
             for u in range(n // P):
                 gathered_words[s0 // P + u] = tile[:, u * P : (u + 1) * P]
 
-        def gather_scales(g):
-            s0, n = sum(SCALE_CUTS[:g]), SCALE_CUTS[g]
+        def gather_scales(s0, n):
             tile = by_vector([P, n], U8, "gs")
             nc.vector.tensor_copy(tile[:], xs[:].bitcast(U8).indirect(offsets[:, s0 // 16 : (s0 + n) // 16]))
-            held["gs", g] = tile
             for u in range(n // P):
                 gathered_scales[s0 // P + u] = tile[:, u * P : (u + 1) * P]
 
         def first(kind, k):
-            if k >= UNITS:
-                return
-            u = unit_at(k)
+            u = ORDER[k]
             name = {"a": "w1", "b": "w3"}[kind]
             acc = bank([P, H], kind)
             nc.tensor.matmul_mx(
@@ -138,8 +106,6 @@ def tile_moe_pke_glu_sigmoid_kernel(
             held[kind, k] = acc
 
         def sigmoid(k):
-            if k >= UNITS:
-                return
             sig = by_scalar([P, H], F32, "sig")
             nc.scalar.activation(
                 sig[:].rearrange("s (v p d) -> s v p d", v=2, d=2),
@@ -149,8 +115,6 @@ def tile_moe_pke_glu_sigmoid_kernel(
             held["sig", k] = sig
 
         def gate(k):
-            if k >= UNITS:
-                return
             h = by_vector([P, H], BF16, "h")
             nc.vector.tensor_tensor(
                 h[:].rearrange("s (v p d) -> s v p d", v=2, d=2),
@@ -162,143 +126,259 @@ def tile_moe_pke_glu_sigmoid_kernel(
 
         def turn(ks):
             turned = bank([P, len(ks), 2, P], "t")
-            for half in reversed(range(len(ks))):
+            for half in range(len(ks)):
                 pairs = held["h", ks[half]][:].bitcast(F32)
                 for v in range(2):
                     nc.tensor.transpose(turned[:, half, v, :], pairs[:, v * P : (v + 1) * P], ident[:])
             held["t", ks] = turned
 
-        def collect(ks):
-            ht = by_scalar([P, 4 * P * len(ks)], BF16, "ht")
+        def collect(ks, engine):
+            ht = (by_vector if engine == "V" else by_scalar)([P, 4 * P * len(ks)], BF16, "ht")
             dst = ht[:].bitcast(F32).rearrange("p (a s v) -> p a s v", a=len(ks), v=2)
-            nc.scalar.copy(dst, held["t", ks][:].rearrange("p a v s -> p a s v"))
+            src = held["t", ks][:].rearrange("p a v s -> p a s v")
+            if engine == "V":
+                nc.vector.tensor_copy(dst, src)
+            else:
+                nc.scalar.copy(dst, src)
             held["ht", ks] = ht
 
         def quantise(ks):
             codes = by_vector([P, P * len(ks)], U32, "codes")
             scales = keep.tile([P, P * len(ks)], U8, name="scales%d" % ks[0], align_bytes=64)
             nc.vector.quantize_mx(codes[:].bitcast(FP8X4), scales[:], held["ht", ks][:])
-            for c, k in enumerate(ks):
-                held["q", k] = (codes[:, c * P : (c + 1) * P], scales[:, c * P : (c + 1) * P])
+            held["q", ks] = (codes, scales)
 
-        def second(g, half, ks):
-            if ks[0] % 2 == 0:
-                held["y", g, half] = bank([P, 2, 2 * P], "y")
-            y = held["y", g, half]
+        def second(ks, half):
+            codes, scales = held["q", ks]
+            y = bank([P, 2, len(ks) * P], "y")
+            whole = len(ks) == 2 and ORDER[ks[0]] // 2 == ORDER[ks[1]] // 2
+            cuts = [(ks[0], 0, 2 * P)] if whole else [(k, c * P, (c + 1) * P) for c, k in enumerate(ks)]
             for j in range(2):
                 t = 2 * half + j
-                for k in ks:
-                    codes, scales = held["q", k]
-                    e = unit_at(k) // 2
+                for k, c0, c1 in cuts:
+                    e = ORDER[k] // 2
                     nc.tensor.matmul_mx(
-                        y[:, j, k % 2 * P : (k % 2 + 1) * P],
+                        y[:, j, c0:c1],
                         lhsT=words["w2", e][:, t * 256 : (t + 1) * 256].bitcast(FP4X4),
                         lhsT_scale=planes["w2", e][:, t * P : (t + 1) * P],
-                        rhs=codes.bitcast(FP8X4),
-                        rhs_scale=scales,
+                        rhs=codes[:, c0:c1].bitcast(FP8X4),
+                        rhs_scale=scales[:, c0:c1],
                         start=True,
                         stop=True,
                     )
+            held["y", ks, half] = y
+
+        def empty(ks, half, engine):
+            new_tile = by_vector if engine == "V" else by_scalar
+            y = held["y", ks, half]
+            if len(ks) == 2 and ORDER[ks[0]] // 2 == ORDER[ks[1]] // 2:
+                result = new_tile([P, 2, 2 * P], F32, "result")
+                held["result", ks, half] = result
+                dst, src = result[:], y[:]
+            elif len(ks) == 2:
+                result = new_tile([P, 2, 2, P], F32, "result")
+                held["result", ks, half] = result
+                dst = result[:].rearrange("p j m (e c) -> p j m e c", e=2)
+                src = y[:].rearrange("p j (e m c) -> p j m e c", e=2, c=64)
+            else:
+                both = (ks[0] // 2 * 2, ks[0] // 2 * 2 + 1)
+                if ("result", both, half) not in held:
+                    held["result", both, half] = new_tile([P, 2, 2, P], F32, "result")
+                dst = held["result", both, half][:, :, :, 64 * (ks[0] % 2) : 64 * (ks[0] % 2 + 1)]
+                src = y[:].rearrange("p j (m c) -> p j m c", c=64)
+            if engine == "V":
+                nc.vector.tensor_copy(dst, src)
+            else:
+                nc.scalar.copy(dst, src)
 
         rows = out.rearrange("(t p) (m c) -> p t m c", p=P, m=R)
 
-        def empty(g, half, engine):
-            u = unit_at(2 * g)
-            ranks = slice(2 * (u % 2), 2 * (u % 2) + 2)
-            cols = slice(64 * (u // 2), 64 * (u // 2 + 2))
-            src = held["y", g, half][:].rearrange("p j (e m c) -> p j m e c", e=2, c=64)
-            if engine == "V":
-                result = by_vector([P, 2, 2, P], F32, "result")
-                nc.vector.tensor_copy(result[:].rearrange("p j m (e c) -> p j m e c", e=2), src)
-            else:
-                result = by_scalar([P, 2, 2, P], F32, "result")
-                nc.scalar.copy(result[:].rearrange("p j m (e c) -> p j m e c", e=2), src)
+        def store_bank(ks, half):
+            e, side = divmod(ORDER[ks[0]], 2)
             for j in range(2):
-                nc.sync.dma_start(rows[:, 2 * half + j, ranks, cols], result[:, j])
+                if ORDER[ks[1]] // 2 == e:
+                    nc.sync.dma_start(
+                        rows[:, 2 * half + j, :, 64 * e : 64 * (e + 1)],
+                        held["result", ks, half][:, j].rearrange("p (m c) -> p m c", c=64),
+                    )
+                    continue
+                nc.sync.dma_start(
+                    rows[:, 2 * half + j, 2 * side : 2 * side + 2, 64 * e : 64 * (e + 2)],
+                    held["result", ks, half][:, j],
+                )
 
-        pair = [(2 * g, 2 * g + 1) for g in range(PAIRS)]
-        blank = keep.tile([P, 4 * P], BF16, name="blank", align_bytes=64)
-        blank_codes = keep.tile([P, P], U32, name="blank_codes", align_bytes=64)
-        blank_scales = keep.tile([P, P], U8, name="blank_scales", align_bytes=64)
-        nc.gpsimd.memset(blank[:], 0.0)
-        nc.vector.quantize_mx(blank_codes[:].bitcast(FP8X4), blank_scales[:], blank[:])
-        gather_scales(0)
-        unread = bank([P, H], "unread")
-        for n in range(WARM):
-            nc.tensor.matmul_mx(
-                unread[:],
-                lhsT=blank_codes[:].bitcast(FP8X4),
-                lhsT_scale=blank_scales[:],
-                rhs=words["w1", 0].bitcast(FP4X4),
-                rhs_scale=held["gs", 0][:, 0:512],
-                start=True,
-                stop=True,
-            )
-        for name, e0, e1 in LATER:
-            load_words(name, e0, e1)
-            if (name, e0) == ("w2", 0):
-                load_scales([sync] * 4, "w2", w2_plane, 0, E)
-            if (name, e0) == ("w3", 2):
-                load_scales([sync] * 4, "w3", late_plane, 2, E)
-        gather_scales(1)
-        def sigmoids(ks):
-            for k in ks:
-                first("a", k)
-            for k in ks:
-                sigmoid(k)
+        offsets = keep.tile([P, S // 16], U16, name="offsets")
+        xs = keep.tile([P, T // 4], I32, name="xs", align_bytes=64)
+        xw = keep.tile([P, T], I32, name="xw", align_bytes=64)
+        ident = keep.tile([P, P], F32, name="ident", align_bytes=64)
 
-        def both_halves(g, ks):
-            second(g, 0, ks)
-            second(g, 1, ks)
+        def load_token_scales():
+            nc.vector.memset(xs[:], 0)
+            for j in range(4):
+                nc.sync.dma_start(xs[j:P:32, :], x_scales[0, j:16:4, :].bitcast(I32))
 
-        gather_words(0)
-        gather_words(1)
-        sigmoids(range(0, 4))
-        gather_words(2)
-        gather_scales(2)
-        for k in range(4):
-            first("b", k)
-        sigmoids(range(4, 8))
-        for k in range(4):
-            gate(k)
-        gather_words(3)
-        for k in pair[2]:
-            first("b", k)
-        for g in range(2):
-            turn(pair[g])
-            collect(pair[g])
-        for k in pair[2]:
-            gate(k)
-        ready = [0, 1]
-        for g in range(2, PAIRS - 1):
-            for done in ready:
-                quantise(pair[done])
-            for k in pair[g + 1]:
-                first("b", k)
-            sigmoids(range(2 * g + 4, 2 * g + 6))
-            turn(pair[g])
-            collect(pair[g])
-            for done in ready:
-                both_halves(done, pair[done])
-            for k in pair[g + 1]:
-                gate(k)
-            if g < PAIRS - 2:
-                for done in ready:
-                    empty(done, 0, "V")
-                    empty(done, 1, "A")
-            ready = [g]
-        g = PAIRS - 1
-        last = [(k,) for k in pair[g]]
-        quantise(pair[g - 1])
-        empty(g - 2, 0, "A")
-        empty(g - 2, 1, "V")
-        for ks in last:
-            turn(ks)
-            collect(ks)
-        both_halves(g - 1, pair[g - 1])
-        for ks in last:
-            quantise(ks)
-            both_halves(g, ks)
-        for done in (g - 1, g):
-            empty(done, 0, "A")
-            empty(done, 1, "V")
+        def load_token_words(t0, t1):
+            nc.sync.dma_start(xw[:, t0:t1], x_words[0].rearrange("p t r -> p (t r)").bitcast(I32)[:, t0:t1])
+
+        def warm_operand():
+            numbers = keep.tile([P, 2, 256], BF16, name="numbers", align_bytes=64)
+            source = words["w1", 0].bitcast(U32).unsqueeze(1).to_broadcast([P, 2, 256])
+            nc.scalar.activation(numbers[:], source, SIGMOID, scale=2.0**-31)
+            held["numbers"] = numbers
+
+        def warm_up(passes):
+            codes = by_vector([P, P], U32, "warm_codes")
+            scales = keep.tile([P, P], U8, name="warm_scales", align_bytes=64)
+            numbers = held["numbers"][:].rearrange("p a w -> p (a w)")
+            nc.vector.quantize_mx(codes[:].bitcast(FP8X4), scales[:], numbers)
+            unread = bank([P, H], "unread")
+            for n in range(passes):
+                nc.tensor.matmul_mx(
+                    unread[:],
+                    lhsT=codes[:].bitcast(FP8X4),
+                    lhsT_scale=scales[:],
+                    rhs=words["w1", 0].bitcast(FP4X4),
+                    rhs_scale=words["w1", 0][:, 512:1024],
+                    start=True,
+                    stop=True,
+                )
+
+        nc.sync.dma_start(offsets[:], offs)
+        load_words("w1", 0, 1)
+        load_token_words(0, 512)
+        load_token_scales()
+        load_token_words(512, T)
+        make_identity(nc, ident[:])
+        for name, e0, e1 in (("w1", 0, 6), ("w3", 0, 2), ("w3", 2, 6), ("w2", 0, 6)):
+            clear_plane(name, e0, e1)
+        warm_operand()
+        load_scales("w1", 0, 6, nc.sync)
+        load_words("w1", 1, 2)
+        load_words("w3", 0, 2)
+        load_scales("w3", 0, 2, nc.sync)
+        load_words("w1", 2, 4)
+        load_words("w3", 2, 4)
+        load_scales("w3", 2, 6, nc.sync)
+        load_words("w1", 4, 6)
+        load_words("w2", 0, 2)
+        load_scales("w2", 0, 6, nc.sync)
+        load_words("w3", 4, 6)
+        load_words("w2", 2, 6)
+        gather_scales(0, 384)
+        warm_up(3)
+        gather_scales(384, 640)
+        gather_words(0, 256)
+        gather_words(256, 256)
+        gather_words(512, 256)
+        gather_words(768, 384)
+        first("a", 0)
+        sigmoid(0)
+        first("a", 2)
+        sigmoid(2)
+        first("a", 1)
+        sigmoid(1)
+        first("a", 3)
+        sigmoid(3)
+        first("b", 0)
+        gate(0)
+        first("b", 2)
+        gate(2)
+        first("b", 1)
+        gate(1)
+        first("b", 3)
+        gate(3)
+        gather_scales(1024, 512)
+        gather_words(1152, 384)
+        first("a", 4)
+        sigmoid(4)
+        first("a", 5)
+        sigmoid(5)
+        first("a", 6)
+        sigmoid(6)
+        first("a", 7)
+        first("b", 4)
+        first("b", 5)
+        turn((0, 1))
+        collect((0, 1), "A")
+        quantise((0, 1))
+        turn((2, 3))
+        collect((2, 3), "A")
+        sigmoid(7)
+        quantise((2, 3))
+        gate(4)
+        gate(5)
+        first("b", 6)
+        gate(6)
+        first("b", 7)
+        gate(7)
+        first("a", 8)
+        sigmoid(8)
+        first("a", 9)
+        sigmoid(9)
+        second((0, 1), 0)
+        empty((0, 1), 0, "A")
+        second((0, 1), 1)
+        store_bank((0, 1), 0)
+        empty((0, 1), 1, "A")
+        second((2, 3), 0)
+        store_bank((0, 1), 1)
+        second((2, 3), 1)
+        empty((2, 3), 1, "V")
+        turn((4, 5))
+        collect((4, 5), "A")
+        empty((2, 3), 0, "A")
+        quantise((4, 5))
+        first("b", 8)
+        store_bank((2, 3), 0)
+        store_bank((2, 3), 1)
+        gate(8)
+        first("b", 9)
+        gate(9)
+        turn((6, 7))
+        collect((6, 7), "A")
+        quantise((6, 7))
+        first("a", 10)
+        sigmoid(10)
+        first("a", 11)
+        sigmoid(11)
+        second((4, 5), 0)
+        empty((4, 5), 0, "A")
+        second((4, 5), 1)
+        store_bank((4, 5), 0)
+        empty((4, 5), 1, "V")
+        first("b", 10)
+        store_bank((4, 5), 1)
+        gate(10)
+        first("b", 11)
+        gate(11)
+        turn((8, 9))
+        collect((8, 9), "A")
+        quantise((8, 9))
+        second((6, 7), 0)
+        empty((6, 7), 0, "A")
+        second((6, 7), 1)
+        store_bank((6, 7), 0)
+        empty((6, 7), 1, "V")
+        turn((10,))
+        store_bank((6, 7), 1)
+        collect((10,), "A")
+        quantise((10,))
+        turn((11,))
+        collect((11,), "A")
+        quantise((11,))
+        second((8, 9), 0)
+        empty((8, 9), 0, "A")
+        second((8, 9), 1)
+        store_bank((8, 9), 0)
+        empty((8, 9), 1, "V")
+        second((10,), 0)
+        store_bank((8, 9), 1)
+        empty((10,), 0, "A")
+        second((10,), 1)
+        empty((10,), 1, "V")
+        second((11,), 0)
+        empty((11,), 0, "A")
+        second((11,), 1)
+        store_bank((10, 11), 0)
+        empty((11,), 1, "V")
+        store_bank((10, 11), 1)

@@ -22,7 +22,7 @@ P = 128
 UNITS = S // P
 VECTOR_TILES = 40
 SCALAR_TILES = 30
-ORDER = (0, 2, 1, 3, 4, 6, 5, 7, 8, 10, 9, 11)
+ORDER = (0, 1, 2, 3, 4, 5, 6, 7, 8, 10, 9, 11)
 
 
 def tile_moe_pke_glu_sigmoid_kernel(
@@ -273,18 +273,18 @@ def tile_moe_pke_glu_sigmoid_kernel(
         gather_words(768, 384)
         first("a", 0)
         sigmoid(0)
-        first("a", 2)
-        sigmoid(2)
         first("a", 1)
         sigmoid(1)
+        first("a", 2)
+        sigmoid(2)
         first("a", 3)
         sigmoid(3)
         first("b", 0)
         gate(0)
-        first("b", 2)
-        gate(2)
         first("b", 1)
         gate(1)
+        first("b", 2)
+        gate(2)
         first("b", 3)
         gate(3)
         gather_scales(1024, 512)

from contextlib import ExitStack

import concourse.mybir as mybir
from concourse.masks import make_identity

K, T, E, C, H, N, R = 512, 2560, 6, 256, 512, 512, 4
S = E * C
FLOPS = 2 * S * (2 * K * H + H * N)

F32 = mybir.dt.float32
BF16 = mybir.dt.bfloat16
I32 = mybir.dt.int32
U32 = mybir.dt.uint32
U16 = mybir.dt.uint16
U8 = mybir.dt.uint8
FP8X4 = mybir.dt.float8_e4m3fn_x4
FP4X4 = mybir.dt.float4_e2m1fn_x4
SIGMOID = mybir.ActivationFunctionType.Sigmoid
MULT = mybir.AluOpType.mult

P = 128
UNITS = S // P
VECTOR_TILES = 40
SCALAR_TILES = 30
ORDER = (0, 1, 2, 3, 4, 5, 6, 7, 8, 10, 9, 11)


def tile_moe_pke_glu_sigmoid_kernel(
    tc, x_words, x_scales, w1_words, w1_scales, w3_words, w3_scales, w2_words, w2_scales, offs, out
):
    nc = tc.nc
    with ExitStack() as ctx:
        keep = ctx.enter_context(tc.tile_pool(name="keep", bufs=1))
        line = ctx.enter_context(tc.tile_pool(name="line", bufs=1))
        psum = ctx.enter_context(tc.psum_pool(name="psum", bufs=8))

        def by_vector(shape, dtype, name):
            return line.tile(shape, dtype, name=name, tag="vector", bufs=VECTOR_TILES, align_bytes=64)

        def by_scalar(shape, dtype, name):
            return line.tile(shape, dtype, name=name, tag="scalar", bufs=SCALAR_TILES, align_bytes=64)

        def bank(shape, name):
            return psum.tile(shape, F32, name=name, tag="bank")

        dram_words = {"w1": w1_words, "w3": w3_words, "w2": w2_words}
        dram_scales = {"w1": w1_scales, "w3": w3_scales, "w2": w2_scales}
        words = {}
        planes = {}
        cleared = {}
        held = {}
        gathered_words = {}
        gathered_scales = {}

        def load_words(name, e0, e1):
            tile = keep.tile([P, (e1 - e0) * 1024], U8, name="%s_words%d" % (name, e0), align_bytes=64)
            nc.sync.dma_start(
                tile[:].bitcast(I32).rearrange("p (e w) -> p e w", e=e1 - e0),
                dram_words[name][e0:e1, 0].rearrange("e p b -> p e b").bitcast(I32),
            )
            for e in range(e0, e1):
                words[name, e] = tile[:, (e - e0) * 1024 : (e - e0 + 1) * 1024]

        def clear_plane(name, e0, e1):
            tile = keep.tile([P, (e1 - e0) * 512], U8, name="%s_plane%d" % (name, e0), align_bytes=64)
            nc.vector.memset(tile[:].bitcast(I32), 0)
            cleared[name, e0] = tile

        def load_scales(name, e0, e1, queue):
            tile = cleared[name, e0]
            for j in range(4):
                queue.dma_start(
                    tile[j:P:32, :].bitcast(I32).rearrange("p (e w) -> p e w", e=e1 - e0),
                    dram_scales[name][e0:e1, 0, j:16:4, :].rearrange("e q b -> q e b").bitcast(I32),
                )
            for e in range(e0, e1):
                planes[name, e] = tile[:, (e - e0) * 512 : (e - e0 + 1) * 512]

        def gather_words(s0, n):
            tile = by_vector([P, n], I32, "gw")
            nc.vector.tensor_copy(
                tile[:].bitcast(U32), xw[:].bitcast(U32).indirect(offsets[:, s0 // 16 : (s0 + n) // 16])
            )
            for u in range(n // P):
                gathered_words[s0 // P + u] = tile[:, u * P : (u + 1) * P]

        def gather_scales(s0, n):
            tile = by_vector([P, n], U8, "gs")
            nc.vector.tensor_copy(tile[:], xs[:].bitcast(U8).indirect(offsets[:, s0 // 16 : (s0 + n) // 16]))
            for u in range(n // P):
                gathered_scales[s0 // P + u] = tile[:, u * P : (u + 1) * P]

        def first(kind, k):
            u = ORDER[k]
            name = {"a": "w1", "b": "w3"}[kind]
            acc = bank([P, H], kind)
            nc.tensor.matmul_mx(
                acc[:],
                lhsT=gathered_words[u].bitcast(FP8X4),
                lhsT_scale=gathered_scales[u],
                rhs=words[name, u // 2].bitcast(FP4X4),
                rhs_scale=planes[name, u // 2],
                start=True,
                stop=True,
            )
            held[kind, k] = acc

        def sigmoid(k):
            sig = by_scalar([P, H], F32, "sig")
            nc.scalar.activation(
                sig[:].rearrange("s (v p d) -> s v p d", v=2, d=2),
                held["a", k][:].rearrange("s (p v d) -> s v p d", v=2, d=2),
                SIGMOID,
            )
            held["sig", k] = sig

        def gate(k):
            h = by_vector([P, H], BF16, "h")
            nc.vector.tensor_tensor(
                h[:].rearrange("s (v p d) -> s v p d", v=2, d=2),
                held["b", k][:].rearrange("s (p v d) -> s v p d", v=2, d=2),
                held["sig", k][:].rearrange("s (v p d) -> s v p d", v=2, d=2),
                MULT,
            )
            held["h", k] = h

        def turn(ks):
            turned = bank([P, len(ks), 2, P], "t")
            for half in range(len(ks)):
                pairs = held["h", ks[half]][:].bitcast(F32)
                for v in range(2):
                    nc.tensor.transpose(turned[:, half, v, :], pairs[:, v * P : (v + 1) * P], ident[:])
            held["t", ks] = turned

        def collect(ks, engine):
            ht = (by_vector if engine == "V" else by_scalar)([P, 4 * P * len(ks)], BF16, "ht")
            dst = ht[:].bitcast(F32).rearrange("p (a s v) -> p a s v", a=len(ks), v=2)
            src = held["t", ks][:].rearrange("p a v s -> p a s v")
            if engine == "V":
                nc.vector.tensor_copy(dst, src)
            else:
                nc.scalar.copy(dst, src)
            held["ht", ks] = ht

        def quantise(ks):
            codes = by_vector([P, P * len(ks)], U32, "codes")
            scales = keep.tile([P, P * len(ks)], U8, name="scales%d" % ks[0], align_bytes=64)
            nc.vector.quantize_mx(codes[:].bitcast(FP8X4), scales[:], held["ht", ks][:])
            held["q", ks] = (codes, scales)

        def second(ks, half):
            codes, scales = held["q", ks]
            y = bank([P, 2, len(ks) * P], "y")
            whole = len(ks) == 2 and ORDER[ks[0]] // 2 == ORDER[ks[1]] // 2
            cuts = [(ks[0], 0, 2 * P)] if whole else [(k, c * P, (c + 1) * P) for c, k in enumerate(ks)]
            for j in range(2):
                t = 2 * half + j
                for k, c0, c1 in cuts:
                    e = ORDER[k] // 2
                    nc.tensor.matmul_mx(
                        y[:, j, c0:c1],
                        lhsT=words["w2", e][:, t * 256 : (t + 1) * 256].bitcast(FP4X4),
                        lhsT_scale=planes["w2", e][:, t * P : (t + 1) * P],
                        rhs=codes[:, c0:c1].bitcast(FP8X4),
                        rhs_scale=scales[:, c0:c1],
                        start=True,
                        stop=True,
                    )
            held["y", ks, half] = y

        def empty(ks, half, engine):
            new_tile = by_vector if engine == "V" else by_scalar
            y = held["y", ks, half]
            if len(ks) == 2 and ORDER[ks[0]] // 2 == ORDER[ks[1]] // 2:
                result = new_tile([P, 2, 2 * P], F32, "result")
                held["result", ks, half] = result
                dst, src = result[:], y[:]
            elif len(ks) == 2:
                result = new_tile([P, 2, 2, P], F32, "result")
                held["result", ks, half] = result
                dst = result[:].rearrange("p j m (e c) -> p j m e c", e=2)
                src = y[:].rearrange("p j (e m c) -> p j m e c", e=2, c=64)
            else:
                both = (ks[0] // 2 * 2, ks[0] // 2 * 2 + 1)
                if ("result", both, half) not in held:
                    held["result", both, half] = new_tile([P, 2, 2, P], F32, "result")
                dst = held["result", both, half][:, :, :, 64 * (ks[0] % 2) : 64 * (ks[0] % 2 + 1)]
                src = y[:].rearrange("p j (m c) -> p j m c", c=64)
            if engine == "V":
                nc.vector.tensor_copy(dst, src)
            else:
                nc.scalar.copy(dst, src)

        rows = out.rearrange("(t p) (m c) -> p t m c", p=P, m=R)

        def store_bank(ks, half):
            e, side = divmod(ORDER[ks[0]], 2)
            for j in range(2):
                if ORDER[ks[1]] // 2 == e:
                    nc.sync.dma_start(
                        rows[:, 2 * half + j, :, 64 * e : 64 * (e + 1)],
                        held["result", ks, half][:, j].rearrange("p (m c) -> p m c", c=64),
                    )
                    continue
                nc.sync.dma_start(
                    rows[:, 2 * half + j, 2 * side : 2 * side + 2, 64 * e : 64 * (e + 2)],
                    held["result", ks, half][:, j],
                )

        offsets = keep.tile([P, S // 16], U16, name="offsets")
        xs = keep.tile([P, T // 4], I32, name="xs", align_bytes=64)
        xw = keep.tile([P, T], I32, name="xw", align_bytes=64)
        ident = keep.tile([P, P], F32, name="ident", align_bytes=64)

        def load_token_scales():
            nc.vector.memset(xs[:], 0)
            for j in range(4):
                nc.sync.dma_start(xs[j:P:32, :], x_scales[0, j:16:4, :].bitcast(I32))

        def load_token_words(t0, t1):
            nc.sync.dma_start(xw[:, t0:t1], x_words[0].rearrange("p t r -> p (t r)").bitcast(I32)[:, t0:t1])

        def warm_operand():
            numbers = keep.tile([P, 2, 256], BF16, name="numbers", align_bytes=64)
            source = words["w1", 0].bitcast(U32).unsqueeze(1).to_broadcast([P, 2, 256])
            nc.scalar.activation(numbers[:], source, SIGMOID, scale=2.0**-31)
            held["numbers"] = numbers

        def warm_up(passes):
            codes = by_vector([P, P], U32, "warm_codes")
            scales = keep.tile([P, P], U8, name="warm_scales", align_bytes=64)
            numbers = held["numbers"][:].rearrange("p a w -> p (a w)")
            nc.vector.quantize_mx(codes[:].bitcast(FP8X4), scales[:], numbers)
            unread = bank([P, H], "unread")
            for n in range(passes):
                nc.tensor.matmul_mx(
                    unread[:],
                    lhsT=codes[:].bitcast(FP8X4),
                    lhsT_scale=scales[:],
                    rhs=words["w1", 0].bitcast(FP4X4),
                    rhs_scale=words["w1", 0][:, 512:1024],
                    start=True,
                    stop=True,
                )

        nc.sync.dma_start(offsets[:], offs)
        load_words("w1", 0, 1)
        load_token_words(0, 512)
        load_token_scales()
        load_token_words(512, T)
        make_identity(nc, ident[:])
        for name, e0, e1 in (("w1", 0, 6), ("w3", 0, 2), ("w3", 2, 6), ("w2", 0, 6)):
            clear_plane(name, e0, e1)
        warm_operand()
        load_scales("w1", 0, 6, nc.sync)
        load_words("w1", 1, 2)
        load_words("w3", 0, 2)
        load_scales("w3", 0, 2, nc.sync)
        load_words("w1", 2, 4)
        load_words("w3", 2, 4)
        load_scales("w3", 2, 6, nc.sync)
        load_words("w1", 4, 6)
        load_words("w2", 0, 2)
        load_scales("w2", 0, 6, nc.sync)
        load_words("w3", 4, 6)
        load_words("w2", 2, 6)
        gather_scales(0, 384)
        warm_up(3)
        gather_scales(384, 640)
        gather_words(0, 256)
        gather_words(256, 256)
        gather_words(512, 256)
        gather_words(768, 384)
        first("a", 0)
        sigmoid(0)
        first("a", 1)
        sigmoid(1)
        first("a", 2)
        sigmoid(2)
        first("a", 3)
        sigmoid(3)
        first("b", 0)
        gate(0)
        first("b", 1)
        gate(1)
        first("b", 2)
        gate(2)
        first("b", 3)
        gate(3)
        gather_scales(1024, 512)
        gather_words(1152, 384)
        first("a", 4)
        sigmoid(4)
        first("a", 5)
        sigmoid(5)
        first("a", 6)
        sigmoid(6)
        first("a", 7)
        first("b", 4)
        first("b", 5)
        turn((0, 1))
        collect((0, 1), "A")
        quantise((0, 1))
        turn((2, 3))
        collect((2, 3), "A")
        sigmoid(7)
        quantise((2, 3))
        gate(4)
        gate(5)
        first("b", 6)
        gate(6)
        first("b", 7)
        gate(7)
        first("a", 8)
        sigmoid(8)
        first("a", 9)
        sigmoid(9)
        second((0, 1), 0)
        empty((0, 1), 0, "A")
        second((0, 1), 1)
        store_bank((0, 1), 0)
        empty((0, 1), 1, "A")
        second((2, 3), 0)
        store_bank((0, 1), 1)
        second((2, 3), 1)
        empty((2, 3), 1, "V")
        turn((4, 5))
        collect((4, 5), "A")
        empty((2, 3), 0, "A")
        quantise((4, 5))
        first("b", 8)
        store_bank((2, 3), 0)
        store_bank((2, 3), 1)
        gate(8)
        first("b", 9)
        gate(9)
        turn((6, 7))
        collect((6, 7), "A")
        quantise((6, 7))
        first("a", 10)
        sigmoid(10)
        first("a", 11)
        sigmoid(11)
        second((4, 5), 0)
        empty((4, 5), 0, "A")
        second((4, 5), 1)
        store_bank((4, 5), 0)
        empty((4, 5), 1, "V")
        first("b", 10)
        store_bank((4, 5), 1)
        gate(10)
        first("b", 11)
        gate(11)
        turn((8, 9))
        collect((8, 9), "A")
        quantise((8, 9))
        second((6, 7), 0)
        empty((6, 7), 0, "A")
        second((6, 7), 1)
        store_bank((6, 7), 0)
        empty((6, 7), 1, "V")
        turn((10,))
        store_bank((6, 7), 1)
        collect((10,), "A")
        quantise((10,))
        turn((11,))
        collect((11,), "A")
        quantise((11,))
        second((8, 9), 0)
        empty((8, 9), 0, "A")
        second((8, 9), 1)
        store_bank((8, 9), 0)
        empty((8, 9), 1, "V")
        second((10,), 0)
        store_bank((8, 9), 1)
        empty((10,), 0, "A")
        second((10,), 1)
        empty((10,), 1, "V")
        second((11,), 0)
        empty((11,), 0, "A")
        second((11,), 1)
        store_bank((10, 11), 0)
        empty((11,), 1, "V")
        store_bank((10, 11), 1)
